import numpy as np
import ml_dtypes


def mxq(x, axis, fmt="e4m3"):
    dtype, down = {"e4m3": (ml_dtypes.float8_e4m3fn, 7), "e5m2": (ml_dtypes.float8_e5m2, 14)}[fmt]
    v = np.moveaxis(np.asarray(x, np.float32).astype(ml_dtypes.bfloat16).astype(np.float64), axis, -1)
    blocks = v.reshape(v.shape[:-1] + (-1, 32))
    amax = np.abs(blocks).max(-1, keepdims=True)
    byte = np.maximum(np.where(amax > 0, np.frexp(amax)[1] - 1 + 127, 0) - down, 1)
    scale = np.exp2(byte - 127.0)
    codes = (blocks / scale).astype(np.float32).astype(dtype).astype(np.float64)
    return np.moveaxis((codes * scale).reshape(v.shape), -1, axis)


WIDE = False


def mx_kscale(k):
    if not WIDE:
        return np.ones(k)
    levels = np.array([10, -10, 5, -5, 0])
    if k % 512:
        return np.exp2(np.random.permutation(np.resize(levels, k // 32))).repeat(32)
    a = np.empty((k // 512, 16))
    for p in range(k // 512):
        a[p, :8] = np.random.permutation(np.resize(levels, 8))
        for g in range(8):
            far = levels[np.abs(levels - a[p, g]) >= 10]
            a[p, g + 8] = far[np.random.randint(len(far))]
    return np.exp2(a.ravel()).repeat(32)


def f64(x):
    return np.asarray(x).astype(np.float64)


def striped(idx):
    return np.tile(idx.reshape(-1, 16).T, (8, 1)).astype(np.uint16)


def unstriped(offs):
    return offs[:16].T.reshape(-1).astype(np.int64)


def gelu(v):
    return 0.5 * v * (1.0 + np.tanh(np.sqrt(2.0 / np.pi) * (v + 0.044715 * v**3)))


K, T, S, N = 512, 4096, 2048, 256


def setup_inputs():
    n = np.random.standard_normal
    s = mx_kscale(K)[:, None]
    return {
        "xT": (n((K, S)) * s).astype(np.float32),
        "w": (n((K, N)) / np.sqrt(K) / s).astype(np.float32),
        "b": (0.3 * n((N, 1))).astype(np.float32),
        "gate": np.tile(np.random.uniform(0.2, 1.0, S), (N, 1)).astype(np.float32),
        "offs": striped(np.sort(np.random.permutation(T)[:S])),
    }


def reference(xT, w, b, gate, offs):
    idx = unstriped(offs)
    xq = mxq(f64(xT), 0, "e4m3")
    y = mxq(f64(w), 0, "e4m3").T @ xq
    y = gelu(y + f64(b))
    out = np.zeros((N, T))
    out[:, idx] = f64(gate) * y
    return out

@@ -1,0 +1,163 @@
+from contextlib import ExitStack
+
+import concourse.mybir as mybir
+
+K, T, S, N = 512, 4096, 2048, 256
+FLOPS = 2 * K * S * N
+BYTES = 4 * (K * S + K * N + N + S + N * T) + 2 * S
+
+F32 = mybir.dt.float32
+BF16 = mybir.dt.bfloat16
+U32 = mybir.dt.uint32
+U16 = mybir.dt.uint16
+U8 = mybir.dt.uint8
+FP8X4 = mybir.dt.float8_e4m3fn_x4
+GELU = mybir.ActivationFunctionType.Gelu_apprx_tanh
+MULT = mybir.AluOpType.mult
+
+P = 128
+PACK = 4
+CHUNK = 512
+CHUNKS = S // CHUNK
+GROUP = 256
+BLOCKS = N // P
+
+
+def tile_picked_place_lin_gelu_srt_l_kernel(tc, xT, w, b, gate, offs, out):
+    nc = tc.nc
+    with ExitStack() as ctx:
+        lists = ctx.enter_context(tc.tile_pool(name="lists", bufs=1))
+        keep = ctx.enter_context(tc.tile_pool(name="keep", bufs=1))
+        ring = ctx.enter_context(tc.tile_pool(name="ring", bufs=2))
+        psum = ctx.enter_context(tc.psum_pool(name="psum", bufs=1))
+
+        offsets = lists.tile([P, S // 16], U16, name="offsets")
+
+        x_hbm = xT.rearrange("(p t) s -> p t s", t=PACK)
+        w_hbm = w.rearrange("(p t) m -> p t m", t=PACK)
+
+        loads = [(0, 256), (256, 256), (512, 512), (1024, 512), (1536, 512)]
+        raw = {c0: keep.tile([P, PACK, n], F32, name="raw%d" % c0) for c0, n in loads}
+        codes = [keep.tile([P, CHUNK], U32, name="codes%d" % c, align_bytes=64) for c in range(CHUNKS)]
+        scales = [keep.tile([P, CHUNK], U8, name="scales%d" % c, align_bytes=64) for c in range(CHUNKS)]
+        values = [[keep.tile([P, CHUNK], F32, name="values%d_%d" % (c, k)) for k in range(BLOCKS)] for c in range(CHUNKS)]
+        sums = [[psum.tile([P, CHUNK], F32, name="sums%d_%d" % (c, k)) for k in range(BLOCKS)] for c in range(CHUNKS)]
+        gates = [keep.tile([P, CHUNK], F32, name="gate%d" % c) for c in range(CHUNKS)]
+        w_raw = keep.tile([P, PACK, N], F32, name="w_raw")
+        w_grouped = keep.tile([P, N * PACK], BF16, name="w_grouped", align_bytes=64)
+        w_codes = keep.tile([P, N], U32, name="w_codes", align_bytes=64)
+        w_scales = keep.tile([P, N], U8, name="w_scales", align_bytes=64)
+        bias = [keep.tile([P, 1], F32, name="bias%d" % k) for k in range(BLOCKS)]
+        windows = [keep.tile([P, T], F32, name="window%d" % k) for k in range(BLOCKS)]
+        small = keep.tile([P, 2], F32, name="small")
+
+        def load_x(c0):
+            n = raw[c0].shape[2]
+            nc.sync.dma_start(raw[c0][:], x_hbm[:, :, c0 : c0 + n])
+
+        def load_gate(c):
+            nc.sync.dma_start(gates[c][:], gate[0:P, c * CHUNK : (c + 1) * CHUNK])
+
+        load_x(0)
+        nc.sync.dma_start(w_raw[:], w_hbm)
+        load_x(256)
+        nc.sync.dma_start(offsets[:], offs)
+        load_gate(0)
+        for c in range(1, CHUNKS):
+            load_x(c * CHUNK)
+            load_gate(c)
+        for k in range(BLOCKS):
+            nc.scalar.dma_start(bias[k][:], b[k * P : (k + 1) * P, :])
+
+        nc.gpsimd.memset(small[:, 0:1], 0.0)
+        nc.scalar.activation(out=small[:, 1:2], in_=small[:, 0:1], func=GELU)
+
+        def clear(k):
+            for q in range(4):
+                nc.vector.memset(windows[k][:, q * 1024 : (q + 1) * 1024], 0.0)
+
+        def interleave(src, dst, engines):
+            n = dst.shape[1] // PACK // len(engines)
+            for i, engine in enumerate(engines):
+                source = src[:, :, i * n : (i + 1) * n].rearrange("p t (c i) -> p c t i", i=4)
+                target = dst[:, PACK * i * n : PACK * (i + 1) * n].rearrange("p (c i t) -> p c t i", i=4, t=PACK)
+                if engine == "V":
+                    nc.vector.tensor_copy(out=target, in_=source)
+                else:
+                    nc.scalar.copy(out=target, in_=source)
+
+        grouped = {}
+
+        def spread(g, engines):
+            c0 = g * GROUP
+            start = c0 if c0 in raw else c0 - GROUP
+            grouped[g] = ring.tile([P, GROUP * PACK], BF16, name="grouped", align_bytes=64)
+            interleave(raw[start][:, :, c0 - start : c0 - start + GROUP], grouped[g], engines)
+
+        def quantize(g):
+            c, a = divmod(g * GROUP, CHUNK)
+            nc.vector.quantize_mx(
+                out=codes[c][:, a : a + GROUP].bitcast(FP8X4), scales=scales[c][:, a : a + GROUP], in_=grouped[g][:]
+            )
+
+        def layer(c, k, a=0, n=CHUNK):
+            mine = slice(k * P, (k + 1) * P)
+            cols = slice(a, a + n)
+            nc.tensor.matmul_mx(
+                out=sums[c][k][:, cols],
+                lhsT=w_codes[:, mine].bitcast(FP8X4),
+                lhsT_scale=w_scales[:, mine],
+                rhs=codes[c][:, cols].bitcast(FP8X4),
+                rhs_scale=scales[c][:, cols],
+                start=True,
+                stop=True,
+            )
+            nc.scalar.activation(out=values[c][k][:, cols], in_=sums[c][k][:, cols], func=GELU, bias=bias[k][:])
+
+        def place(c, k):
+            n = CHUNK // 16
+            nc.vector.tensor_tensor(
+                windows[k][:].indirect(offsets[:, c * n : (c + 1) * n]), values[c][k][:], gates[c][:], MULT
+            )
+
+        def store(k, c0, c1):
+            nc.sync.dma_start(out[k * P : (k + 1) * P, c0:c1], windows[k][:, c0:c1])
+
+        clear(0)
+        spread(0, "SV")
+        interleave(w_raw, w_grouped, "SS")
+        quantize(0)
+        spread(1, "SS")
+        nc.vector.quantize_mx(out=w_codes[:].bitcast(FP8X4), scales=w_scales[:], in_=w_grouped[:])
+        quantize(1)
+        clear(1)
+        for k in range(BLOCKS):
+            for a in (0, GROUP):
+                layer(0, k, a, GROUP)
+        spread(2, "VS")
+        spread(3, "SS")
+        quantize(2)
+        quantize(3)
+        place(0, 0)
+        layer(1, 0)
+        place(1, 0)
+        store(0, 0, 1024)
+        place(0, 1)
+        layer(1, 1)
+        place(1, 1)
+        store(1, 0, 1024)
+        spread(4, "S")
+        spread(5, "S")
+        quantize(4)
+        quantize(5)
+        layer(2, 0)
+        layer(2, 1)
+        spread(6, "VS")
+        spread(7, "VS")
+        quantize(6)
+        quantize(7)
+        for k in range(BLOCKS):
+            place(2, k)
+            layer(3, k)
+            place(3, k)
+            store(k, 1024, T)

@@ -21,6 +21,7 @@ CHUNK = 512
 CHUNKS = S // CHUNK
 GROUP = 256
 BLOCKS = N // P
+STORES = {1: (0, 1024), 2: (1024, 1536), 3: (1536, T)}
 
 
 def tile_picked_place_lin_gelu_srt_l_kernel(tc, xT, w, b, gate, offs, out):
@@ -28,7 +29,6 @@ def tile_picked_place_lin_gelu_srt_l_kernel(tc, xT, w, b, gate, offs, out):
     with ExitStack() as ctx:
         lists = ctx.enter_context(tc.tile_pool(name="lists", bufs=1))
         keep = ctx.enter_context(tc.tile_pool(name="keep", bufs=1))
-        ring = ctx.enter_context(tc.tile_pool(name="ring", bufs=2))
         psum = ctx.enter_context(tc.psum_pool(name="psum", bufs=1))
 
         offsets = lists.tile([P, S // 16], U16, name="offsets")
@@ -36,8 +36,9 @@ def tile_picked_place_lin_gelu_srt_l_kernel(tc, xT, w, b, gate, offs, out):
         x_hbm = xT.rearrange("(p t) s -> p t s", t=PACK)
         w_hbm = w.rearrange("(p t) m -> p t m", t=PACK)
 
-        loads = [(0, 256), (256, 256), (512, 512), (1024, 512), (1536, 512)]
+        loads = [(0, 256), (256, 256), (512, 256), (768, 256), (1024, 512), (1536, 512)]
         raw = {c0: keep.tile([P, PACK, n], F32, name="raw%d" % c0) for c0, n in loads}
+        grouped = [keep.tile([P, GROUP * PACK], BF16, name="grouped%d" % g, align_bytes=64) for g in range(S // GROUP)]
         codes = [keep.tile([P, CHUNK], U32, name="codes%d" % c, align_bytes=64) for c in range(CHUNKS)]
         scales = [keep.tile([P, CHUNK], U8, name="scales%d" % c, align_bytes=64) for c in range(CHUNKS)]
         values = [[keep.tile([P, CHUNK], F32, name="values%d_%d" % (c, k)) for k in range(BLOCKS)] for c in range(CHUNKS)]
@@ -47,7 +48,7 @@ def tile_picked_place_lin_gelu_srt_l_kernel(tc, xT, w, b, gate, offs, out):
         w_grouped = keep.tile([P, N * PACK], BF16, name="w_grouped", align_bytes=64)
         w_codes = keep.tile([P, N], U32, name="w_codes", align_bytes=64)
         w_scales = keep.tile([P, N], U8, name="w_scales", align_bytes=64)
-        bias = [keep.tile([P, 1], F32, name="bias%d" % k) for k in range(BLOCKS)]
+        bias = keep.tile([P, BLOCKS], F32, name="bias")
         windows = [keep.tile([P, T], F32, name="window%d" % k) for k in range(BLOCKS)]
         small = keep.tile([P, 2], F32, name="small")
 
@@ -58,41 +59,42 @@ def tile_picked_place_lin_gelu_srt_l_kernel(tc, xT, w, b, gate, offs, out):
         def load_gate(c):
             nc.sync.dma_start(gates[c][:], gate[0:P, c * CHUNK : (c + 1) * CHUNK])
 
-        load_x(0)
         nc.sync.dma_start(w_raw[:], w_hbm)
+        load_x(0)
         load_x(256)
         nc.sync.dma_start(offsets[:], offs)
         load_gate(0)
-        for c in range(1, CHUNKS):
-            load_x(c * CHUNK)
-            load_gate(c)
-        for k in range(BLOCKS):
-            nc.scalar.dma_start(bias[k][:], b[k * P : (k + 1) * P, :])
+        load_x(512)
+        load_x(768)
+        load_x(1024)
+        load_gate(1)
+        load_x(1536)
+        load_gate(2)
+        load_gate(3)
+        nc.scalar.dma_start(bias[:], b.rearrange("(k p) o -> p (k o)", p=P))
 
         nc.gpsimd.memset(small[:, 0:1], 0.0)
         nc.scalar.activation(out=small[:, 1:2], in_=small[:, 0:1], func=GELU)
 
         def clear(k):
-            for q in range(4):
-                nc.vector.memset(windows[k][:, q * 1024 : (q + 1) * 1024], 0.0)
+            for q in range(T // CHUNK):
+                nc.vector.memset(windows[k][:, q * CHUNK : (q + 1) * CHUNK], 0.0)
 
-        def interleave(src, dst, engines):
-            n = dst.shape[1] // PACK // len(engines)
-            for i, engine in enumerate(engines):
-                source = src[:, :, i * n : (i + 1) * n].rearrange("p t (c i) -> p c t i", i=4)
-                target = dst[:, PACK * i * n : PACK * (i + 1) * n].rearrange("p (c i t) -> p c t i", i=4, t=PACK)
-                if engine == "V":
-                    nc.vector.tensor_copy(out=target, in_=source)
-                else:
-                    nc.scalar.copy(out=target, in_=source)
+        def interleave(engine, src, dst, a, n):
+            source = src[:, :, a : a + n].rearrange("p t (c i) -> p c t i", i=4)
+            target = dst.rearrange("p (c i t) -> p c t i", i=4, t=PACK)
+            if engine == "V":
+                nc.vector.tensor_copy(out=target, in_=source)
+            else:
+                nc.scalar.copy(out=target, in_=source)
 
-        grouped = {}
-
-        def spread(g, engines):
+        def spread(g, on_vector=0):
             c0 = g * GROUP
             start = c0 if c0 in raw else c0 - GROUP
-            grouped[g] = ring.tile([P, GROUP * PACK], BF16, name="grouped", align_bytes=64)
-            interleave(raw[start][:, :, c0 - start : c0 - start + GROUP], grouped[g], engines)
+            a = c0 - start
+            if on_vector:
+                interleave("V", raw[start], grouped[g][:, 0 : PACK * on_vector], a, on_vector)
+            interleave("S", raw[start], grouped[g][:, PACK * on_vector :], a + on_vector, GROUP - on_vector)
 
         def quantize(g):
             c, a = divmod(g * GROUP, CHUNK)
@@ -100,7 +102,7 @@ def tile_picked_place_lin_gelu_srt_l_kernel(tc, xT, w, b, gate, offs, out):
                 out=codes[c][:, a : a + GROUP].bitcast(FP8X4), scales=scales[c][:, a : a + GROUP], in_=grouped[g][:]
             )
 
-        def layer(c, k, a=0, n=CHUNK):
+        def multiply(c, k, a=0, n=CHUNK):
             mine = slice(k * P, (k + 1) * P)
             cols = slice(a, a + n)
             nc.tensor.matmul_mx(
@@ -112,7 +114,10 @@ def tile_picked_place_lin_gelu_srt_l_kernel(tc, xT, w, b, gate, offs, out):
                 start=True,
                 stop=True,
             )
-            nc.scalar.activation(out=values[c][k][:, cols], in_=sums[c][k][:, cols], func=GELU, bias=bias[k][:])
+
+        def activate(c, k, a=0, n=CHUNK):
+            cols = slice(a, a + n)
+            nc.scalar.activation(out=values[c][k][:, cols], in_=sums[c][k][:, cols], func=GELU, bias=bias[:, k : k + 1])
 
         def place(c, k):
             n = CHUNK // 16
@@ -124,40 +129,32 @@ def tile_picked_place_lin_gelu_srt_l_kernel(tc, xT, w, b, gate, offs, out):
             nc.sync.dma_start(out[k * P : (k + 1) * P, c0:c1], windows[k][:, c0:c1])
 
         clear(0)
-        spread(0, "SV")
-        interleave(w_raw, w_grouped, "SS")
-        quantize(0)
-        spread(1, "SS")
+        interleave("S", w_raw, w_grouped[:], 0, N)
         nc.vector.quantize_mx(out=w_codes[:].bitcast(FP8X4), scales=w_scales[:], in_=w_grouped[:])
-        quantize(1)
-        clear(1)
-        for k in range(BLOCKS):
-            for a in (0, GROUP):
-                layer(0, k, a, GROUP)
-        spread(2, "VS")
-        spread(3, "SS")
-        quantize(2)
-        quantize(3)
+        for g in range(2):
+            spread(g, on_vector=160)
+            quantize(g)
+            multiply(0, 0, g * GROUP, GROUP)
+            activate(0, 0, g * GROUP, GROUP)
+        multiply(0, 1)
         place(0, 0)
-        layer(1, 0)
-        place(1, 0)
-        store(0, 0, 1024)
-        place(0, 1)
-        layer(1, 1)
-        place(1, 1)
-        store(1, 0, 1024)
-        spread(4, "S")
-        spread(5, "S")
-        quantize(4)
-        quantize(5)
-        layer(2, 0)
-        layer(2, 1)
-        spread(6, "VS")
-        spread(7, "VS")
-        quantize(6)
-        quantize(7)
-        for k in range(BLOCKS):
-            place(2, k)
-            layer(3, k)
-            place(3, k)
-            store(k, 1024, T)
+        spread(2)
+        quantize(2)
+        clear(1)
+        for c in range(CHUNKS):
+            if c > 0:
+                activate(c, 0)
+                place(c, 0)
+                store(0, *STORES[c])
+            if c + 1 < CHUNKS:
+                spread(2 * c + 3)
+                quantize(2 * c + 3)
+                for k in range(BLOCKS):
+                    multiply(c + 1, k)
+            activate(c, 1)
+            place(c, 1)
+            if c > 0:
+                store(1, *STORES[c])
+            if c + 2 < CHUNKS:
+                spread(2 * c + 4)
+                quantize(2 * c + 4)

@@ -21,7 +21,8 @@ CHUNK = 512
 CHUNKS = S // CHUNK
 GROUP = 256
 BLOCKS = N // P
-STORES = {1: (0, 1024), 2: (1024, 1536), 3: (1536, T)}
+GROUPS = S // GROUP
+HALF = S // 2
 
 
 def tile_picked_place_lin_gelu_srt_l_kernel(tc, xT, w, b, gate, offs, out):
@@ -36,14 +37,11 @@ def tile_picked_place_lin_gelu_srt_l_kernel(tc, xT, w, b, gate, offs, out):
         x_hbm = xT.rearrange("(p t) s -> p t s", t=PACK)
         w_hbm = w.rearrange("(p t) m -> p t m", t=PACK)
 
-        loads = [(0, 256), (256, 256), (512, 256), (768, 256), (1024, 512), (1536, 512)]
-        raw = {c0: keep.tile([P, PACK, n], F32, name="raw%d" % c0) for c0, n in loads}
-        grouped = [keep.tile([P, GROUP * PACK], BF16, name="grouped%d" % g, align_bytes=64) for g in range(S // GROUP)]
+        raw = [keep.tile([P, PACK, GROUP], F32, name="raw%d" % g, tag="slot%d" % g) for g in range(GROUPS)]
+        grouped = [keep.tile([P, GROUP * PACK], BF16, name="grouped%d" % g, align_bytes=64) for g in range(GROUPS)]
         codes = [keep.tile([P, CHUNK], U32, name="codes%d" % c, align_bytes=64) for c in range(CHUNKS)]
         scales = [keep.tile([P, CHUNK], U8, name="scales%d" % c, align_bytes=64) for c in range(CHUNKS)]
-        values = [[keep.tile([P, CHUNK], F32, name="values%d_%d" % (c, k)) for k in range(BLOCKS)] for c in range(CHUNKS)]
-        sums = [[psum.tile([P, CHUNK], F32, name="sums%d_%d" % (c, k)) for k in range(BLOCKS)] for c in range(CHUNKS)]
-        gates = [keep.tile([P, CHUNK], F32, name="gate%d" % c) for c in range(CHUNKS)]
+        gates = keep.tile([P, 2 * CHUNK], F32, name="gates")
         w_raw = keep.tile([P, PACK, N], F32, name="w_raw")
         w_grouped = keep.tile([P, N * PACK], BF16, name="w_grouped", align_bytes=64)
         w_codes = keep.tile([P, N], U32, name="w_codes", align_bytes=64)
@@ -51,50 +49,52 @@ def tile_picked_place_lin_gelu_srt_l_kernel(tc, xT, w, b, gate, offs, out):
         bias = keep.tile([P, BLOCKS], F32, name="bias")
         windows = [keep.tile([P, T], F32, name="window%d" % k) for k in range(BLOCKS)]
         small = keep.tile([P, 2], F32, name="small")
+        last_values = keep.tile([P, 2 * CHUNK], F32, name="last_values")
+        sums = {(c, k): psum.tile([P, CHUNK], F32, name="sums%d_%d" % (c, k)) for c in range(CHUNKS) for k in range(BLOCKS)}
 
-        def load_x(c0):
-            n = raw[c0].shape[2]
-            nc.sync.dma_start(raw[c0][:], x_hbm[:, :, c0 : c0 + n])
+        def load_x(g):
+            nc.sync.dma_start(raw[g][:], x_hbm[:, :, g * GROUP : (g + 1) * GROUP])
+
+        def gate_of(c, n=CHUNK):
+            a = (c % 2) * CHUNK
+            return gates[:, a : a + n]
 
         def load_gate(c):
-            nc.sync.dma_start(gates[c][:], gate[0:P, c * CHUNK : (c + 1) * CHUNK])
+            nc.sync.dma_start(gate_of(c), gate[0:P, c * CHUNK : (c + 1) * CHUNK])
 
         nc.sync.dma_start(w_raw[:], w_hbm)
         load_x(0)
-        load_x(256)
+        load_x(1)
         nc.sync.dma_start(offsets[:], offs)
         load_gate(0)
-        load_x(512)
-        load_x(768)
-        load_x(1024)
+        for g in (2, 3, 4):
+            load_x(g)
         load_gate(1)
-        load_x(1536)
-        load_gate(2)
-        load_gate(3)
+        for g in (5, 6, 7):
+            load_x(g)
         nc.scalar.dma_start(bias[:], b.rearrange("(k p) o -> p (k o)", p=P))
 
         nc.gpsimd.memset(small[:, 0:1], 0.0)
         nc.scalar.activation(out=small[:, 1:2], in_=small[:, 0:1], func=GELU)
 
-        def clear(k):
-            for q in range(T // CHUNK):
-                nc.vector.memset(windows[k][:, q * CHUNK : (q + 1) * CHUNK], 0.0)
+        strip = windows[0][:, 0:CHUNK]
+
+        def clear(k, first):
+            for q in range(first, T // CHUNK):
+                nc.vector.tensor_copy(out=windows[k][:, q * CHUNK : (q + 1) * CHUNK], in_=strip)
 
         def interleave(engine, src, dst, a, n):
             source = src[:, :, a : a + n].rearrange("p t (c i) -> p c t i", i=4)
-            target = dst.rearrange("p (c i t) -> p c t i", i=4, t=PACK)
+            target = dst[:, PACK * a : PACK * (a + n)].rearrange("p (c i t) -> p c t i", i=4, t=PACK)
             if engine == "V":
                 nc.vector.tensor_copy(out=target, in_=source)
             else:
                 nc.scalar.copy(out=target, in_=source)
 
         def spread(g, on_vector=0):
-            c0 = g * GROUP
-            start = c0 if c0 in raw else c0 - GROUP
-            a = c0 - start
             if on_vector:
-                interleave("V", raw[start], grouped[g][:, 0 : PACK * on_vector], a, on_vector)
-            interleave("S", raw[start], grouped[g][:, PACK * on_vector :], a + on_vector, GROUP - on_vector)
+                interleave("V", raw[g], grouped[g], 0, on_vector)
+            interleave("S", raw[g], grouped[g], on_vector, GROUP - on_vector)
 
         def quantize(g):
             c, a = divmod(g * GROUP, CHUNK)
@@ -106,7 +106,7 @@ def tile_picked_place_lin_gelu_srt_l_kernel(tc, xT, w, b, gate, offs, out):
             mine = slice(k * P, (k + 1) * P)
             cols = slice(a, a + n)
             nc.tensor.matmul_mx(
-                out=sums[c][k][:, cols],
+                out=sums[c, k][:, cols],
                 lhsT=w_codes[:, mine].bitcast(FP8X4),
                 lhsT_scale=w_scales[:, mine],
                 rhs=codes[c][:, cols].bitcast(FP8X4),
@@ -115,46 +115,61 @@ def tile_picked_place_lin_gelu_srt_l_kernel(tc, xT, w, b, gate, offs, out):
                 stop=True,
             )
 
-        def activate(c, k, a=0, n=CHUNK):
-            cols = slice(a, a + n)
-            nc.scalar.activation(out=values[c][k][:, cols], in_=sums[c][k][:, cols], func=GELU, bias=bias[:, k : k + 1])
+        def activate(c, k, target, a=0, n=CHUNK):
+            nc.scalar.activation(out=target, in_=sums[c, k][:, a : a + n], func=GELU, bias=bias[:, k : k + 1])
 
-        def place(c, k):
-            n = CHUNK // 16
-            nc.vector.tensor_tensor(
-                windows[k][:].indirect(offsets[:, c * n : (c + 1) * n]), values[c][k][:], gates[c][:], MULT
-            )
+        def values_in(tag):
+            return keep.tile([P, CHUNK], F32, name="values_" + tag, tag=tag)
+
+        def place(c, k, values, n=CHUNK):
+            a = c * CHUNK // 16
+            nc.vector.tensor_tensor(windows[k][:].indirect(offsets[:, a : a + n // 16]), values, gate_of(c, n), MULT)
 
         def store(k, c0, c1):
             nc.sync.dma_start(out[k * P : (k + 1) * P, c0:c1], windows[k][:, c0:c1])
 
-        clear(0)
-        interleave("S", w_raw, w_grouped[:], 0, N)
+        def finish(c, k, tag):
+            values = values_in(tag)
+            activate(c, k, values[:])
+            place(c, k, values[:])
+
+        def prepare(g):
+            spread(g)
+            quantize(g)
+            if g % 2:
+                for k in range(BLOCKS):
+                    multiply(g // 2, k)
+
+        nc.vector.memset(strip, 0.0)
+        clear(0, 1)
+        interleave("S", w_raw, w_grouped, 0, N)
         nc.vector.quantize_mx(out=w_codes[:].bitcast(FP8X4), scales=w_scales[:], in_=w_grouped[:])
-        for g in range(2):
-            spread(g, on_vector=160)
+        first = values_in("first")
+        for g, on_vector in ((0, 96), (1, 160)):
+            spread(g, on_vector)
             quantize(g)
             multiply(0, 0, g * GROUP, GROUP)
-            activate(0, 0, g * GROUP, GROUP)
+            activate(0, 0, first[:, g * GROUP : (g + 1) * GROUP], g * GROUP, GROUP)
         multiply(0, 1)
-        place(0, 0)
-        spread(2)
-        quantize(2)
-        clear(1)
-        for c in range(CHUNKS):
-            if c > 0:
-                activate(c, 0)
-                place(c, 0)
-                store(0, *STORES[c])
-            if c + 1 < CHUNKS:
-                spread(2 * c + 3)
-                quantize(2 * c + 3)
-                for k in range(BLOCKS):
-                    multiply(c + 1, k)
-            activate(c, 1)
-            place(c, 1)
-            if c > 0:
-                store(1, *STORES[c])
-            if c + 2 < CHUNKS:
-                spread(2 * c + 4)
-                quantize(2 * c + 4)
+        clear(1, 0)
+        place(0, 0, first[:])
+        prepare(2)
+        prepare(3)
+        finish(0, 1, "slot3")
+        load_gate(2)
+        prepare(4)
+        finish(1, 0, "slot4")
+        store(0, 0, HALF)
+        prepare(5)
+        finish(1, 1, "slot5")
+        load_gate(3)
+        store(1, 0, HALF)
+        prepare(6)
+        prepare(7)
+        finish(2, 0, "slot7")
+        finish(3, 0, "slot6")
+        store(0, HALF, T)
+        for c in (2, 3):
+            activate(c, 1, last_values[:, (c - 2) * CHUNK : (c - 1) * CHUNK])
+        place(2, 1, last_values[:], 2 * CHUNK)
+        store(1, HALF, T)

@@ -37,8 +37,8 @@ def tile_picked_place_lin_gelu_srt_l_kernel(tc, xT, w, b, gate, offs, out):
         x_hbm = xT.rearrange("(p t) s -> p t s", t=PACK)
         w_hbm = w.rearrange("(p t) m -> p t m", t=PACK)
 
-        raw = [keep.tile([P, PACK, GROUP], F32, name="raw%d" % g, tag="slot%d" % g) for g in range(GROUPS)]
-        grouped = [keep.tile([P, GROUP * PACK], BF16, name="grouped%d" % g, align_bytes=64) for g in range(GROUPS)]
+        raw = [keep.tile([P, PACK, CHUNK], F32, name="raw%d" % c, tag="slot%d" % c, align_bytes=64) for c in range(CHUNKS)]
+        grouped = [keep.tile([P, CHUNK * PACK], BF16, name="grouped%d" % c, align_bytes=64) for c in range(CHUNKS)]
         codes = [keep.tile([P, CHUNK], U32, name="codes%d" % c, align_bytes=64) for c in range(CHUNKS)]
         scales = [keep.tile([P, CHUNK], U8, name="scales%d" % c, align_bytes=64) for c in range(CHUNKS)]
         gates = keep.tile([P, 2 * CHUNK], F32, name="gates")
@@ -50,10 +50,9 @@ def tile_picked_place_lin_gelu_srt_l_kernel(tc, xT, w, b, gate, offs, out):
         windows = [keep.tile([P, T], F32, name="window%d" % k) for k in range(BLOCKS)]
         small = keep.tile([P, 2], F32, name="small")
         last_values = keep.tile([P, 2 * CHUNK], F32, name="last_values")
-        sums = {(c, k): psum.tile([P, CHUNK], F32, name="sums%d_%d" % (c, k)) for c in range(CHUNKS) for k in range(BLOCKS)}
 
-        def load_x(g):
-            nc.sync.dma_start(raw[g][:], x_hbm[:, :, g * GROUP : (g + 1) * GROUP])
+        def load_x(c):
+            nc.sync.dma_start(raw[c][:], x_hbm[:, :, c * CHUNK : (c + 1) * CHUNK])
 
         def gate_of(c, n=CHUNK):
             a = (c % 2) * CHUNK
@@ -62,16 +61,14 @@ def tile_picked_place_lin_gelu_srt_l_kernel(tc, xT, w, b, gate, offs, out):
         def load_gate(c):
             nc.sync.dma_start(gate_of(c), gate[0:P, c * CHUNK : (c + 1) * CHUNK])
 
-        nc.sync.dma_start(w_raw[:], w_hbm)
         load_x(0)
-        load_x(1)
+        nc.sync.dma_start(w_raw[:], w_hbm)
         nc.sync.dma_start(offsets[:], offs)
         load_gate(0)
-        for g in (2, 3, 4):
-            load_x(g)
+        load_x(1)
+        load_x(2)
         load_gate(1)
-        for g in (5, 6, 7):
-            load_x(g)
+        load_x(3)
         nc.scalar.dma_start(bias[:], b.rearrange("(k p) o -> p (k o)", p=P))
 
         nc.gpsimd.memset(small[:, 0:1], 0.0)
@@ -91,22 +88,17 @@ def tile_picked_place_lin_gelu_srt_l_kernel(tc, xT, w, b, gate, offs, out):
             else:
                 nc.scalar.copy(out=target, in_=source)
 
-        def spread(g, on_vector=0):
-            if on_vector:
-                interleave("V", raw[g], grouped[g], 0, on_vector)
-            interleave("S", raw[g], grouped[g], on_vector, GROUP - on_vector)
-
-        def quantize(g):
-            c, a = divmod(g * GROUP, CHUNK)
+        def quantize(words, plane, src, a, n):
             nc.vector.quantize_mx(
-                out=codes[c][:, a : a + GROUP].bitcast(FP8X4), scales=scales[c][:, a : a + GROUP], in_=grouped[g][:]
+                out=words[:, a : a + n].bitcast(FP8X4), scales=plane[:, a : a + n], in_=src[:, PACK * a : PACK * (a + n)]
             )
 
-        def multiply(c, k, a=0, n=CHUNK):
+        def multiply(c, k, bank, a=0, n=CHUNK):
             mine = slice(k * P, (k + 1) * P)
             cols = slice(a, a + n)
+            sums = psum.tile([P, n], F32, name="sums%d_%d_%d" % (c, k, a), tag="bank%d" % bank)
             nc.tensor.matmul_mx(
-                out=sums[c, k][:, cols],
+                out=sums[:],
                 lhsT=w_codes[:, mine].bitcast(FP8X4),
                 lhsT_scale=w_scales[:, mine],
                 rhs=codes[c][:, cols].bitcast(FP8X4),
@@ -114,12 +106,13 @@ def tile_picked_place_lin_gelu_srt_l_kernel(tc, xT, w, b, gate, offs, out):
                 start=True,
                 stop=True,
             )
+            return sums
 
-        def activate(c, k, target, a=0, n=CHUNK):
-            nc.scalar.activation(out=target, in_=sums[c, k][:, a : a + n], func=GELU, bias=bias[:, k : k + 1])
+        def activate(k, sums, target):
+            nc.scalar.activation(out=target, in_=sums[:], func=GELU, bias=bias[:, k : k + 1])
 
         def values_in(tag):
-            return keep.tile([P, CHUNK], F32, name="values_" + tag, tag=tag)
+            return keep.tile([P, CHUNK], F32, name="values_" + tag, tag=tag, align_bytes=64)
 
         def place(c, k, values, n=CHUNK):
             a = c * CHUNK // 16
@@ -128,48 +121,62 @@ def tile_picked_place_lin_gelu_srt_l_kernel(tc, xT, w, b, gate, offs, out):
         def store(k, c0, c1):
             nc.sync.dma_start(out[k * P : (k + 1) * P, c0:c1], windows[k][:, c0:c1])
 
+        sums = {}
+
         def finish(c, k, tag):
             values = values_in(tag)
-            activate(c, k, values[:])
+            activate(k, sums[c, k], values[:])
             place(c, k, values[:])
 
-        def prepare(g):
-            spread(g)
-            quantize(g)
-            if g % 2:
-                for k in range(BLOCKS):
-                    multiply(g // 2, k)
+        def prepare(c, a, n=GROUP):
+            interleave("S", raw[c], grouped[c], a, n)
+            quantize(codes[c], scales[c], grouped[c], a, n)
+
+        def products(c):
+            for k in range(BLOCKS):
+                sums[c, k] = multiply(c, k, BLOCKS * c + k)
 
         nc.vector.memset(strip, 0.0)
         clear(0, 1)
-        interleave("S", w_raw, w_grouped, 0, N)
-        nc.vector.quantize_mx(out=w_codes[:].bitcast(FP8X4), scales=w_scales[:], in_=w_grouped[:])
+        interleave("V", raw[0], grouped[0], 0, GROUP)
+        interleave("V", raw[0], grouped[0], GROUP, 64)
+        interleave("S", raw[0], grouped[0], GROUP + 64, GROUP - 64)
+        for a in (0, GROUP):
+            quantize(codes[0], scales[0], grouped[0], a, GROUP)
+        interleave("V", w_raw, w_grouped, 0, 80)
+        interleave("S", w_raw, w_grouped, 80, P - 80)
+        quantize(w_codes, w_scales, w_grouped, 0, P)
+        interleave("S", w_raw, w_grouped, P, P)
+        quantize(w_codes, w_scales, w_grouped, P, P)
         first = values_in("first")
-        for g, on_vector in ((0, 96), (1, 160)):
-            spread(g, on_vector)
-            quantize(g)
-            multiply(0, 0, g * GROUP, GROUP)
-            activate(0, 0, first[:, g * GROUP : (g + 1) * GROUP], g * GROUP, GROUP)
-        multiply(0, 1)
+        for a, bank in ((0, 0), (GROUP, 7)):
+            activate(0, multiply(0, 0, bank, a, GROUP), first[:, a : a + GROUP])
+        sums[0, 1] = multiply(0, 1, 1)
         clear(1, 0)
         place(0, 0, first[:])
-        prepare(2)
-        prepare(3)
-        finish(0, 1, "slot3")
+        prepare(1, 0)
+        aside = keep.tile([P, CHUNK * PACK], BF16, name="aside", tag="first", align_bytes=64)
+        interleave("V", raw[1], aside, GROUP, P)
+        quantize(codes[1], scales[1], aside, GROUP, P)
+        prepare(1, GROUP + P, P)
+        products(1)
+        finish(0, 1, "slot1")
         load_gate(2)
-        prepare(4)
-        finish(1, 0, "slot4")
+        prepare(2, 0)
+        finish(1, 0, "values1_0")
         store(0, 0, HALF)
-        prepare(5)
-        finish(1, 1, "slot5")
+        prepare(2, GROUP)
+        products(2)
+        finish(1, 1, "slot2")
         load_gate(3)
         store(1, 0, HALF)
-        prepare(6)
-        prepare(7)
-        finish(2, 0, "slot7")
-        finish(3, 0, "slot6")
+        prepare(3, 0)
+        prepare(3, GROUP)
+        products(3)
+        finish(2, 0, "slot3")
+        finish(3, 0, "values3_0")
         store(0, HALF, T)
         for c in (2, 3):
-            activate(c, 1, last_values[:, (c - 2) * CHUNK : (c - 1) * CHUNK])
+            activate(1, sums[c, 1], last_values[:, (c - 2) * CHUNK : (c - 1) * CHUNK])
         place(2, 1, last_values[:], 2 * CHUNK)
         store(1, HALF, T)

@@ -61,11 +61,11 @@ def tile_picked_place_lin_gelu_srt_l_kernel(tc, xT, w, b, gate, offs, out):
         def load_gate(c):
             nc.sync.dma_start(gate_of(c), gate[0:P, c * CHUNK : (c + 1) * CHUNK])
 
-        load_x(0)
         nc.sync.dma_start(w_raw[:], w_hbm)
-        nc.sync.dma_start(offsets[:], offs)
-        load_gate(0)
+        load_x(0)
         load_x(1)
+        load_gate(0)
+        nc.sync.dma_start(offsets[:], offs)
         load_x(2)
         load_gate(1)
         load_x(3)
@@ -128,9 +128,12 @@ def tile_picked_place_lin_gelu_srt_l_kernel(tc, xT, w, b, gate, offs, out):
             activate(k, sums[c, k], values[:])
             place(c, k, values[:])
 
-        def prepare(c, a, n=GROUP):
-            interleave("S", raw[c], grouped[c], a, n)
-            quantize(codes[c], scales[c], grouped[c], a, n)
+        def prepare(c, a, on_vector=0):
+            if on_vector:
+                interleave("V", raw[c], grouped[c], a, on_vector)
+            if on_vector < GROUP:
+                interleave("S", raw[c], grouped[c], a + on_vector, GROUP - on_vector)
+            quantize(codes[c], scales[c], grouped[c], a, GROUP)
 
         def products(c):
             for k in range(BLOCKS):
@@ -138,40 +141,28 @@ def tile_picked_place_lin_gelu_srt_l_kernel(tc, xT, w, b, gate, offs, out):
 
         nc.vector.memset(strip, 0.0)
         clear(0, 1)
-        interleave("V", raw[0], grouped[0], 0, GROUP)
-        interleave("V", raw[0], grouped[0], GROUP, 64)
-        interleave("S", raw[0], grouped[0], GROUP + 64, GROUP - 64)
-        for a in (0, GROUP):
-            quantize(codes[0], scales[0], grouped[0], a, GROUP)
-        interleave("V", w_raw, w_grouped, 0, 80)
-        interleave("S", w_raw, w_grouped, 80, P - 80)
-        quantize(w_codes, w_scales, w_grouped, 0, P)
-        interleave("S", w_raw, w_grouped, P, P)
-        quantize(w_codes, w_scales, w_grouped, P, P)
-        first = values_in("first")
-        for a, bank in ((0, 0), (GROUP, 7)):
-            activate(0, multiply(0, 0, bank, a, GROUP), first[:, a : a + GROUP])
-        sums[0, 1] = multiply(0, 1, 1)
+        interleave("S", w_raw, w_grouped, 0, N)
+        quantize(w_codes, w_scales, w_grouped, 0, N)
+        for c in range(2):
+            prepare(c, 0, GROUP)
+            prepare(c, GROUP)
+            products(c)
         clear(1, 0)
-        place(0, 0, first[:])
-        prepare(1, 0)
-        aside = keep.tile([P, CHUNK * PACK], BF16, name="aside", tag="first", align_bytes=64)
-        interleave("V", raw[1], aside, GROUP, P)
-        quantize(codes[1], scales[1], aside, GROUP, P)
-        prepare(1, GROUP + P, P)
-        products(1)
-        finish(0, 1, "slot1")
+        both = keep.tile([P, BLOCKS, CHUNK], F32, name="both", tag="slot1", align_bytes=64)
+        for k in range(BLOCKS):
+            activate(k, sums[0, k], both[:, k, :])
+            place(0, k, both[:, k, :])
         load_gate(2)
-        prepare(2, 0)
         finish(1, 0, "values1_0")
         store(0, 0, HALF)
+        prepare(2, 0)
         prepare(2, GROUP)
         products(2)
         finish(1, 1, "slot2")
         load_gate(3)
         store(1, 0, HALF)
         prepare(3, 0)
-        prepare(3, GROUP)
+        prepare(3, GROUP, P)
         products(3)
         finish(2, 0, "slot3")
         finish(3, 0, "values3_0")

@@ -17,12 +17,15 @@ MULT = mybir.AluOpType.mult
 
 P = 128
 PACK = 4
+STRIPE = 16
 CHUNK = 512
 CHUNKS = S // CHUNK
-GROUP = 256
+GROUP = CHUNK // 2
 BLOCKS = N // P
-GROUPS = S // GROUP
 HALF = S // 2
+RUN = 4
+BIAS_PITCH = 8
+ON_VECTOR = {(0, 0): GROUP, (1, 0): GROUP, (1, GROUP): 64, (3, GROUP): GROUP // 2}
 
 
 def tile_picked_place_lin_gelu_srt_l_kernel(tc, xT, w, b, gate, offs, out):
@@ -32,12 +35,12 @@ def tile_picked_place_lin_gelu_srt_l_kernel(tc, xT, w, b, gate, offs, out):
         keep = ctx.enter_context(tc.tile_pool(name="keep", bufs=1))
         psum = ctx.enter_context(tc.psum_pool(name="psum", bufs=1))
 
-        offsets = lists.tile([P, S // 16], U16, name="offsets")
+        offsets = lists.tile([P, S // STRIPE], U16, name="offsets")
 
         x_hbm = xT.rearrange("(p t) s -> p t s", t=PACK)
         w_hbm = w.rearrange("(p t) m -> p t m", t=PACK)
 
-        raw = [keep.tile([P, PACK, CHUNK], F32, name="raw%d" % c, tag="slot%d" % c, align_bytes=64) for c in range(CHUNKS)]
+        raw = [keep.tile([P, PACK, CHUNK], F32, name="raw%d" % c, align_bytes=64) for c in range(CHUNKS)]
         grouped = [keep.tile([P, CHUNK * PACK], BF16, name="grouped%d" % c, align_bytes=64) for c in range(CHUNKS)]
         codes = [keep.tile([P, CHUNK], U32, name="codes%d" % c, align_bytes=64) for c in range(CHUNKS)]
         scales = [keep.tile([P, CHUNK], U8, name="scales%d" % c, align_bytes=64) for c in range(CHUNKS)]
@@ -46,9 +49,9 @@ def tile_picked_place_lin_gelu_srt_l_kernel(tc, xT, w, b, gate, offs, out):
         w_grouped = keep.tile([P, N * PACK], BF16, name="w_grouped", align_bytes=64)
         w_codes = keep.tile([P, N], U32, name="w_codes", align_bytes=64)
         w_scales = keep.tile([P, N], U8, name="w_scales", align_bytes=64)
-        bias = keep.tile([P, BLOCKS], F32, name="bias")
+        bias = keep.tile([P, BLOCKS, BIAS_PITCH], F32, name="bias")
         windows = [keep.tile([P, T], F32, name="window%d" % k) for k in range(BLOCKS)]
-        small = keep.tile([P, 2], F32, name="small")
+        warm = keep.tile([P, 2], F32, name="warm")
         last_values = keep.tile([P, 2 * CHUNK], F32, name="last_values")
 
         def load_x(c):
@@ -64,15 +67,15 @@ def tile_picked_place_lin_gelu_srt_l_kernel(tc, xT, w, b, gate, offs, out):
         nc.sync.dma_start(w_raw[:], w_hbm)
         load_x(0)
         load_x(1)
+        nc.sync.dma_start(bias[:, :, 0:1], b.rearrange("(k p) o -> p k o", p=P))
         load_gate(0)
         nc.sync.dma_start(offsets[:], offs)
         load_x(2)
         load_gate(1)
         load_x(3)
-        nc.scalar.dma_start(bias[:], b.rearrange("(k p) o -> p (k o)", p=P))
 
-        nc.gpsimd.memset(small[:, 0:1], 0.0)
-        nc.scalar.activation(out=small[:, 1:2], in_=small[:, 0:1], func=GELU)
+        nc.gpsimd.memset(warm[:, 0:1], 0.0)
+        nc.scalar.activation(out=warm[:, 1:2], in_=warm[:, 0:1], func=GELU)
 
         strip = windows[0][:, 0:CHUNK]
 
@@ -80,94 +83,83 @@ def tile_picked_place_lin_gelu_srt_l_kernel(tc, xT, w, b, gate, offs, out):
             for q in range(first, T // CHUNK):
                 nc.vector.tensor_copy(out=windows[k][:, q * CHUNK : (q + 1) * CHUNK], in_=strip)
 
-        def interleave(engine, src, dst, a, n):
-            source = src[:, :, a : a + n].rearrange("p t (c i) -> p c t i", i=4)
-            target = dst[:, PACK * a : PACK * (a + n)].rearrange("p (c i t) -> p c t i", i=4, t=PACK)
-            if engine == "V":
-                nc.vector.tensor_copy(out=target, in_=source)
-            else:
-                nc.scalar.copy(out=target, in_=source)
+        def interleave(copy, src, dst, a, n):
+            source = src[:, :, a : a + n].rearrange("p t (c i) -> p c t i", i=RUN)
+            target = dst[:, PACK * a : PACK * (a + n)].rearrange("p (c i t) -> p c t i", i=RUN, t=PACK)
+            copy(out=target, in_=source)
 
-        def quantize(words, plane, src, a, n):
+        def quantize(words, scale_bytes, src, a, n):
             nc.vector.quantize_mx(
-                out=words[:, a : a + n].bitcast(FP8X4), scales=plane[:, a : a + n], in_=src[:, PACK * a : PACK * (a + n)]
+                out=words[:, a : a + n].bitcast(FP8X4),
+                scales=scale_bytes[:, a : a + n],
+                in_=src[:, PACK * a : PACK * (a + n)],
             )
 
-        def multiply(c, k, bank, a=0, n=CHUNK):
-            mine = slice(k * P, (k + 1) * P)
-            cols = slice(a, a + n)
-            sums = psum.tile([P, n], F32, name="sums%d_%d_%d" % (c, k, a), tag="bank%d" % bank)
-            nc.tensor.matmul_mx(
-                out=sums[:],
-                lhsT=w_codes[:, mine].bitcast(FP8X4),
-                lhsT_scale=w_scales[:, mine],
-                rhs=codes[c][:, cols].bitcast(FP8X4),
-                rhs_scale=scales[c][:, cols],
-                start=True,
-                stop=True,
-            )
-            return sums
+        def prepare(c, a):
+            on_vector = ON_VECTOR.get((c, a), 0)
+            if on_vector:
+                interleave(nc.vector.tensor_copy, raw[c], grouped[c], a, on_vector)
+            if on_vector < GROUP:
+                interleave(nc.scalar.copy, raw[c], grouped[c], a + on_vector, GROUP - on_vector)
+            quantize(codes[c], scales[c], grouped[c], a, GROUP)
 
-        def activate(k, sums, target):
-            nc.scalar.activation(out=target, in_=sums[:], func=GELU, bias=bias[:, k : k + 1])
+        sums = {}
 
-        def values_in(tag):
-            return keep.tile([P, CHUNK], F32, name="values_" + tag, tag=tag, align_bytes=64)
+        def products(c):
+            for a in (0, GROUP):
+                prepare(c, a)
+            for k in range(BLOCKS):
+                mine = slice(k * P, (k + 1) * P)
+                sums[c, k] = psum.tile([P, CHUNK], F32, name="sums%d_%d" % (c, k))
+                nc.tensor.matmul_mx(
+                    out=sums[c, k][:],
+                    lhsT=w_codes[:, mine].bitcast(FP8X4),
+                    lhsT_scale=w_scales[:, mine],
+                    rhs=codes[c][:].bitcast(FP8X4),
+                    rhs_scale=scales[c][:],
+                    start=True,
+                    stop=True,
+                )
+
+        def activate(c, k, target):
+            nc.scalar.activation(out=target, in_=sums[c, k][:], func=GELU, bias=bias[:, k, 0:1])
 
         def place(c, k, values, n=CHUNK):
-            a = c * CHUNK // 16
-            nc.vector.tensor_tensor(windows[k][:].indirect(offsets[:, a : a + n // 16]), values, gate_of(c, n), MULT)
+            a = c * CHUNK // STRIPE
+            nc.vector.tensor_tensor(windows[k][:].indirect(offsets[:, a : a + n // STRIPE]), values, gate_of(c, n), MULT)
+
+        def finish(c, k, tag=None):
+            name = "values%d_%d" % (c, k)
+            values = keep.tile([P, CHUNK], F32, name=name, tag=tag or name, align_bytes=64)
+            activate(c, k, values[:])
+            place(c, k, values[:])
 
         def store(k, c0, c1):
             nc.sync.dma_start(out[k * P : (k + 1) * P, c0:c1], windows[k][:, c0:c1])
 
-        sums = {}
-
-        def finish(c, k, tag):
-            values = values_in(tag)
-            activate(k, sums[c, k], values[:])
-            place(c, k, values[:])
-
-        def prepare(c, a, on_vector=0):
-            if on_vector:
-                interleave("V", raw[c], grouped[c], a, on_vector)
-            if on_vector < GROUP:
-                interleave("S", raw[c], grouped[c], a + on_vector, GROUP - on_vector)
-            quantize(codes[c], scales[c], grouped[c], a, GROUP)
-
-        def products(c):
-            for k in range(BLOCKS):
-                sums[c, k] = multiply(c, k, BLOCKS * c + k)
-
         nc.vector.memset(strip, 0.0)
         clear(0, 1)
-        interleave("S", w_raw, w_grouped, 0, N)
+        interleave(nc.scalar.copy, w_raw, w_grouped, 0, N)
         quantize(w_codes, w_scales, w_grouped, 0, N)
-        for c in range(2):
-            prepare(c, 0, GROUP)
-            prepare(c, GROUP)
-            products(c)
+        products(0)
+        products(1)
         clear(1, 0)
-        both = keep.tile([P, BLOCKS, CHUNK], F32, name="both", tag="slot1", align_bytes=64)
+
         for k in range(BLOCKS):
-            activate(k, sums[0, k], both[:, k, :])
-            place(0, k, both[:, k, :])
+            finish(0, k)
         load_gate(2)
-        finish(1, 0, "values1_0")
+        finish(1, 0)
         store(0, 0, HALF)
-        prepare(2, 0)
-        prepare(2, GROUP)
         products(2)
-        finish(1, 1, "slot2")
+        finish(1, 1, tag="raw2")
         load_gate(3)
         store(1, 0, HALF)
-        prepare(3, 0)
-        prepare(3, GROUP, P)
+
         products(3)
-        finish(2, 0, "slot3")
-        finish(3, 0, "values3_0")
+        for c in (2, 3):
+            finish(c, 0)
         store(0, HALF, T)
         for c in (2, 3):
-            activate(1, sums[c, 1], last_values[:, (c - 2) * CHUNK : (c - 1) * CHUNK])
+            activate(c, 1, last_values[:, (c - 2) * CHUNK : (c - 1) * CHUNK])
         place(2, 1, last_values[:], 2 * CHUNK)
         store(1, HALF, T)

@@ -16,6 +16,7 @@ GELU = mybir.ActivationFunctionType.Gelu_apprx_tanh
 MULT = mybir.AluOpType.mult
 
 P = 128
+QUAD = 32
 PACK = 4
 STRIPE = 16
 CHUNK = 512
@@ -24,8 +25,6 @@ GROUP = CHUNK // 2
 BLOCKS = N // P
 HALF = S // 2
 RUN = 4
-BIAS_PITCH = 8
-ON_VECTOR = {(0, 0): GROUP, (1, 0): GROUP, (1, GROUP): 64, (3, GROUP): GROUP // 2}
 
 
 def tile_picked_place_lin_gelu_srt_l_kernel(tc, xT, w, b, gate, offs, out):
@@ -40,42 +39,50 @@ def tile_picked_place_lin_gelu_srt_l_kernel(tc, xT, w, b, gate, offs, out):
         x_hbm = xT.rearrange("(p t) s -> p t s", t=PACK)
         w_hbm = w.rearrange("(p t) m -> p t m", t=PACK)
 
-        raw = [keep.tile([P, PACK, CHUNK], F32, name="raw%d" % c, align_bytes=64) for c in range(CHUNKS)]
         grouped = [keep.tile([P, CHUNK * PACK], BF16, name="grouped%d" % c, align_bytes=64) for c in range(CHUNKS)]
         codes = [keep.tile([P, CHUNK], U32, name="codes%d" % c, align_bytes=64) for c in range(CHUNKS)]
         scales = [keep.tile([P, CHUNK], U8, name="scales%d" % c, align_bytes=64) for c in range(CHUNKS)]
-        gates = keep.tile([P, 2 * CHUNK], F32, name="gates")
+        gates = keep.tile([P, 3 * CHUNK], F32, name="gates")
         w_raw = keep.tile([P, PACK, N], F32, name="w_raw")
         w_grouped = keep.tile([P, N * PACK], BF16, name="w_grouped", align_bytes=64)
         w_codes = keep.tile([P, N], U32, name="w_codes", align_bytes=64)
         w_scales = keep.tile([P, N], U8, name="w_scales", align_bytes=64)
-        bias = keep.tile([P, BLOCKS, BIAS_PITCH], F32, name="bias")
+        bias_rows = keep.tile([P, P], F32, name="bias_rows", align_bytes=64)
+        bias = keep.tile([P, P], F32, name="bias", align_bytes=64)
         windows = [keep.tile([P, T], F32, name="window%d" % k) for k in range(BLOCKS)]
-        warm = keep.tile([P, 2], F32, name="warm")
         last_values = keep.tile([P, 2 * CHUNK], F32, name="last_values")
 
-        def load_x(c):
-            nc.sync.dma_start(raw[c][:], x_hbm[:, :, c * CHUNK : (c + 1) * CHUNK])
+        raw = {}
+
+        def load_x(c, a, n):
+            raw[c, a] = keep.tile([P, PACK, n], F32, name="raw%d_%d" % (c, a), align_bytes=64)
+            first = c * CHUNK + a
+            nc.sync.dma_start(raw[c, a][:], x_hbm[:, :, first : first + n])
 
         def gate_of(c, n=CHUNK):
-            a = (c % 2) * CHUNK
+            a = (0, 2, 1, 2)[c] * CHUNK
             return gates[:, a : a + n]
 
         def load_gate(c):
             nc.sync.dma_start(gate_of(c), gate[0:P, c * CHUNK : (c + 1) * CHUNK])
 
         nc.sync.dma_start(w_raw[:], w_hbm)
-        load_x(0)
-        load_x(1)
-        nc.sync.dma_start(bias[:, :, 0:1], b.rearrange("(k p) o -> p k o", p=P))
+        nc.gpsimd.memset(bias_rows[:], 0.0)
+        nc.sync.dma_start(
+            bias_rows[0:P:QUAD, 0 : BLOCKS * QUAD].rearrange("q (k j) -> q k j", j=QUAD),
+            b.rearrange("(k q j) o -> q k (j o)", k=BLOCKS, j=QUAD),
+        )
+        load_x(0, 0, CHUNK)
+        load_x(1, 0, GROUP)
+        load_x(1, GROUP, GROUP)
         load_gate(0)
         nc.sync.dma_start(offsets[:], offs)
-        load_x(2)
+        load_x(2, 0, GROUP)
         load_gate(1)
-        load_x(3)
-
-        nc.gpsimd.memset(warm[:, 0:1], 0.0)
-        nc.scalar.activation(out=warm[:, 1:2], in_=warm[:, 0:1], func=GELU)
+        load_x(2, GROUP, GROUP)
+        load_gate(2)
+        load_x(3, 0, GROUP)
+        load_x(3, GROUP, GROUP)
 
         strip = windows[0][:, 0:CHUNK]
 
@@ -83,10 +90,13 @@ def tile_picked_place_lin_gelu_srt_l_kernel(tc, xT, w, b, gate, offs, out):
             for q in range(first, T // CHUNK):
                 nc.vector.tensor_copy(out=windows[k][:, q * CHUNK : (q + 1) * CHUNK], in_=strip)
 
-        def interleave(copy, src, dst, a, n):
-            source = src[:, :, a : a + n].rearrange("p t (c i) -> p c t i", i=RUN)
+        def interleave(copy, src, dst, at, a, n):
+            source = src[:, :, a - at : a - at + n].rearrange("p t (c i) -> p c t i", i=RUN)
             target = dst[:, PACK * a : PACK * (a + n)].rearrange("p (c i t) -> p c t i", i=RUN, t=PACK)
             copy(out=target, in_=source)
+
+        def weave(copy, c, at, a, n):
+            interleave(copy, raw[c, at], grouped[c], at, a, n)
 
         def quantize(words, scale_bytes, src, a, n):
             nc.vector.quantize_mx(
@@ -95,69 +105,94 @@ def tile_picked_place_lin_gelu_srt_l_kernel(tc, xT, w, b, gate, offs, out):
                 in_=src[:, PACK * a : PACK * (a + n)],
             )
 
-        def prepare(c, a):
-            on_vector = ON_VECTOR.get((c, a), 0)
-            if on_vector:
-                interleave(nc.vector.tensor_copy, raw[c], grouped[c], a, on_vector)
-            if on_vector < GROUP:
-                interleave(nc.scalar.copy, raw[c], grouped[c], a + on_vector, GROUP - on_vector)
+        def quantize_x(c, a):
             quantize(codes[c], scales[c], grouped[c], a, GROUP)
 
         sums = {}
 
-        def products(c):
-            for a in (0, GROUP):
-                prepare(c, a)
-            for k in range(BLOCKS):
-                mine = slice(k * P, (k + 1) * P)
-                sums[c, k] = psum.tile([P, CHUNK], F32, name="sums%d_%d" % (c, k))
-                nc.tensor.matmul_mx(
-                    out=sums[c, k][:],
-                    lhsT=w_codes[:, mine].bitcast(FP8X4),
-                    lhsT_scale=w_scales[:, mine],
-                    rhs=codes[c][:].bitcast(FP8X4),
-                    rhs_scale=scales[c][:],
-                    start=True,
-                    stop=True,
-                )
+        def product(c, k, bank, a=0, n=CHUNK):
+            mine = slice(k * P, (k + 1) * P)
+            sums[c, k, a] = psum.tile([P, CHUNK], F32, name="sums%d_%d_%d" % (c, k, a), tag="bank%d" % bank)
+            nc.tensor.matmul_mx(
+                out=sums[c, k, a][:, 0:n],
+                lhsT=w_codes[:, mine].bitcast(FP8X4),
+                lhsT_scale=w_scales[:, mine],
+                rhs=codes[c][:, a : a + n].bitcast(FP8X4),
+                rhs_scale=scales[c][:, a : a + n],
+                start=True,
+                stop=True,
+            )
 
-        def activate(c, k, target):
-            nc.scalar.activation(out=target, in_=sums[c, k][:], func=GELU, bias=bias[:, k, 0:1])
+        def activate(c, k, target, a=0, n=CHUNK):
+            nc.scalar.activation(out=target, in_=sums[c, k, a][:, 0:n], func=GELU, bias=bias[:, QUAD * k : QUAD * k + 1])
 
         def place(c, k, values, n=CHUNK):
             a = c * CHUNK // STRIPE
             nc.vector.tensor_tensor(windows[k][:].indirect(offsets[:, a : a + n // STRIPE]), values, gate_of(c, n), MULT)
 
-        def finish(c, k, tag=None):
+        vals = {}
+
+        def finish(c, k, firsts, tag=None):
             name = "values%d_%d" % (c, k)
             values = keep.tile([P, CHUNK], F32, name=name, tag=tag or name, align_bytes=64)
-            activate(c, k, values[:])
+            vals[c, k] = values
+            n = CHUNK // len(firsts)
+            for a in firsts:
+                activate(c, k, values[:, a : a + n], a, n)
             place(c, k, values[:])
 
         def store(k, c0, c1):
             nc.sync.dma_start(out[k * P : (k + 1) * P, c0:c1], windows[k][:, c0:c1])
 
+        on_vector, on_scalar = nc.vector.tensor_copy, nc.scalar.copy
+        halves, whole = (0, GROUP), (0,)
+
         nc.vector.memset(strip, 0.0)
         clear(0, 1)
-        interleave(nc.scalar.copy, w_raw, w_grouped, 0, N)
+        nc.scalar.activation(out=windows[1][:, 0 : 3 * CHUNK], in_=windows[0][:, 0 : 3 * CHUNK], func=GELU)
+        nc.vector.transpose(bias[:], bias_rows[:])
+        interleave(on_scalar, w_raw, w_grouped, 0, 0, N)
         quantize(w_codes, w_scales, w_grouped, 0, N)
-        products(0)
-        products(1)
-        clear(1, 0)
 
-        for k in range(BLOCKS):
-            finish(0, k)
-        load_gate(2)
-        finish(1, 0)
+        weave(on_vector, 0, 0, 0, GROUP)
+        weave(on_scalar, 0, 0, GROUP, GROUP)
+        for a, bank in ((0, 0), (GROUP, 1)):
+            quantize_x(0, a)
+            product(0, 0, bank, a, GROUP)
+        product(0, 1, 2)
+        weave(on_vector, 1, 0, 0, GROUP // 2)
+        weave(on_scalar, 1, 0, GROUP // 2, GROUP // 2)
+        quantize_x(1, 0)
+        product(1, 0, 3, 0, GROUP)
+        weave(on_vector, 1, GROUP, GROUP, GROUP)
+        quantize_x(1, GROUP)
+        product(1, 0, 4, GROUP, GROUP)
+        product(1, 1, 5)
+        clear(1, 3)
+
+        finish(0, 0, halves, tag="raw1_0")
+        finish(0, 1, whole)
+        finish(1, 0, halves)
         store(0, 0, HALF)
-        products(2)
-        finish(1, 1, tag="raw2")
+        for a in halves:
+            weave(on_scalar, 2, a, a, GROUP)
+            quantize_x(2, a)
+        product(2, 0, 6)
+        product(2, 1, 7)
+        finish(1, 1, whole, tag="raw2_256")
         load_gate(3)
         store(1, 0, HALF)
 
-        products(3)
-        for c in (2, 3):
-            finish(c, 0)
+        weave(on_scalar, 3, 0, 0, GROUP)
+        quantize_x(3, 0)
+        product(3, 0, 0, 0, GROUP)
+        weave(on_vector, 3, GROUP, GROUP, GROUP // 2)
+        weave(on_scalar, 3, GROUP, GROUP + GROUP // 2, GROUP // 2)
+        quantize_x(3, GROUP)
+        product(3, 0, 1, GROUP, GROUP)
+        product(3, 1, 2)
+        finish(2, 0, whole)
+        finish(3, 0, halves)
         store(0, HALF, T)
         for c in (2, 3):
             activate(c, 1, last_values[:, (c - 2) * CHUNK : (c - 1) * CHUNK])

@@ -16,7 +16,7 @@ GELU = mybir.ActivationFunctionType.Gelu_apprx_tanh
 MULT = mybir.AluOpType.mult
 
 P = 128
-QUAD = 32
+BIAS_PITCH = 8
 PACK = 4
 STRIPE = 16
 CHUNK = 512
@@ -47,8 +47,7 @@ def tile_picked_place_lin_gelu_srt_l_kernel(tc, xT, w, b, gate, offs, out):
         w_grouped = keep.tile([P, N * PACK], BF16, name="w_grouped", align_bytes=64)
         w_codes = keep.tile([P, N], U32, name="w_codes", align_bytes=64)
         w_scales = keep.tile([P, N], U8, name="w_scales", align_bytes=64)
-        bias_rows = keep.tile([P, P], F32, name="bias_rows", align_bytes=64)
-        bias = keep.tile([P, P], F32, name="bias", align_bytes=64)
+        bias = keep.tile([P, BLOCKS, BIAS_PITCH], F32, name="bias")
         windows = [keep.tile([P, T], F32, name="window%d" % k) for k in range(BLOCKS)]
         last_values = keep.tile([P, 2 * CHUNK], F32, name="last_values")
 
@@ -60,25 +59,20 @@ def tile_picked_place_lin_gelu_srt_l_kernel(tc, xT, w, b, gate, offs, out):
             nc.sync.dma_start(raw[c, a][:], x_hbm[:, :, first : first + n])
 
         def gate_of(c, n=CHUNK):
-            a = (0, 2, 1, 2)[c] * CHUNK
+            a = (c + 1) % 3 * CHUNK
             return gates[:, a : a + n]
 
         def load_gate(c):
             nc.sync.dma_start(gate_of(c), gate[0:P, c * CHUNK : (c + 1) * CHUNK])
 
         nc.sync.dma_start(w_raw[:], w_hbm)
-        nc.gpsimd.memset(bias_rows[:], 0.0)
-        nc.sync.dma_start(
-            bias_rows[0:P:QUAD, 0 : BLOCKS * QUAD].rearrange("q (k j) -> q k j", j=QUAD),
-            b.rearrange("(k q j) o -> q k (j o)", k=BLOCKS, j=QUAD),
-        )
         load_x(0, 0, CHUNK)
-        load_x(1, 0, GROUP)
-        load_x(1, GROUP, GROUP)
+        load_x(1, 0, CHUNK)
+        nc.sync.dma_start(bias[:, :, 0:1], b.rearrange("(k p) o -> p k o", p=P))
         load_gate(0)
         nc.sync.dma_start(offsets[:], offs)
-        load_x(2, 0, GROUP)
         load_gate(1)
+        load_x(2, 0, GROUP)
         load_x(2, GROUP, GROUP)
         load_gate(2)
         load_x(3, 0, GROUP)
@@ -124,7 +118,7 @@ def tile_picked_place_lin_gelu_srt_l_kernel(tc, xT, w, b, gate, offs, out):
             )
 
         def activate(c, k, target, a=0, n=CHUNK):
-            nc.scalar.activation(out=target, in_=sums[c, k, a][:, 0:n], func=GELU, bias=bias[:, QUAD * k : QUAD * k + 1])
+            nc.scalar.activation(out=target, in_=sums[c, k, a][:, 0:n], func=GELU, bias=bias[:, k, 0:1])
 
         def place(c, k, values, n=CHUNK):
             a = c * CHUNK // STRIPE
@@ -149,50 +143,51 @@ def tile_picked_place_lin_gelu_srt_l_kernel(tc, xT, w, b, gate, offs, out):
 
         nc.vector.memset(strip, 0.0)
         clear(0, 1)
-        nc.scalar.activation(out=windows[1][:, 0 : 3 * CHUNK], in_=windows[0][:, 0 : 3 * CHUNK], func=GELU)
-        nc.vector.transpose(bias[:], bias_rows[:])
+        nc.scalar.activation(out=windows[1][:, 0:HALF], in_=windows[0][:, 0:HALF], func=GELU)
         interleave(on_scalar, w_raw, w_grouped, 0, 0, N)
         quantize(w_codes, w_scales, w_grouped, 0, N)
 
         weave(on_vector, 0, 0, 0, GROUP)
         weave(on_scalar, 0, 0, GROUP, GROUP)
-        for a, bank in ((0, 0), (GROUP, 1)):
+        for a in halves:
             quantize_x(0, a)
-            product(0, 0, bank, a, GROUP)
-        product(0, 1, 2)
-        weave(on_vector, 1, 0, 0, GROUP // 2)
-        weave(on_scalar, 1, 0, GROUP // 2, GROUP // 2)
+        product(0, 1, 0)
+        product(0, 0, 1)
+        weave(on_vector, 1, 0, 0, GROUP)
         quantize_x(1, 0)
-        product(1, 0, 3, 0, GROUP)
-        weave(on_vector, 1, GROUP, GROUP, GROUP)
+        product(1, 0, 2, 0, GROUP)
+        weave(on_vector, 1, 0, GROUP, GROUP // 2)
+        weave(on_scalar, 1, 0, GROUP + GROUP // 2, GROUP // 2)
         quantize_x(1, GROUP)
-        product(1, 0, 4, GROUP, GROUP)
-        product(1, 1, 5)
-        clear(1, 3)
+        product(1, 0, 3, GROUP, GROUP)
+        product(1, 1, 4)
+        clear(1, 2)
 
-        finish(0, 0, halves, tag="raw1_0")
         finish(0, 1, whole)
-        finish(1, 0, halves)
+        first_values = keep.tile([P, 2 * CHUNK], F32, name="first_values")
+        activate(0, 0, first_values[:, 0:CHUNK])
+        for a in halves:
+            activate(1, 0, first_values[:, CHUNK + a : CHUNK + a + GROUP], a, GROUP)
+        place(0, 0, first_values[:], 2 * CHUNK)
         store(0, 0, HALF)
+        load_gate(3)
         for a in halves:
             weave(on_scalar, 2, a, a, GROUP)
             quantize_x(2, a)
-        product(2, 0, 6)
-        product(2, 1, 7)
+        product(2, 0, 5)
         finish(1, 1, whole, tag="raw2_256")
-        load_gate(3)
         store(1, 0, HALF)
 
-        weave(on_scalar, 3, 0, 0, GROUP)
+        weave(on_vector, 3, 0, 0, GROUP // 4)
+        weave(on_scalar, 3, 0, GROUP // 4, 3 * GROUP // 4)
         quantize_x(3, 0)
-        product(3, 0, 0, 0, GROUP)
-        weave(on_vector, 3, GROUP, GROUP, GROUP // 2)
-        weave(on_scalar, 3, GROUP, GROUP + GROUP // 2, GROUP // 2)
+        weave(on_scalar, 3, GROUP, GROUP, GROUP)
         quantize_x(3, GROUP)
-        product(3, 0, 1, GROUP, GROUP)
-        product(3, 1, 2)
-        finish(2, 0, whole)
-        finish(3, 0, halves)
+        product(3, 0, 0)
+        product(3, 1, 1)
+        finish(2, 0, whole, tag="raw3_256")
+        finish(3, 0, whole)
+        product(2, 1, 0)
         store(0, HALF, T)
         for c in (2, 3):
             activate(c, 1, last_values[:, (c - 2) * CHUNK : (c - 1) * CHUNK])

@@ -16,7 +16,6 @@ GELU = mybir.ActivationFunctionType.Gelu_apprx_tanh
 MULT = mybir.AluOpType.mult
 
 P = 128
-BIAS_PITCH = 8
 PACK = 4
 STRIPE = 16
 CHUNK = 512
@@ -25,6 +24,12 @@ GROUP = CHUNK // 2
 BLOCKS = N // P
 HALF = S // 2
 RUN = 4
+BIAS_PITCH = 8
+GATE_SLOTS = 3
+SCALAR_OF_1 = 128
+VECTOR_OF_3 = 64
+CUT_OF_3 = 384
+SCALAR_CLEARS = 2
 
 
 def tile_picked_place_lin_gelu_srt_l_kernel(tc, xT, w, b, gate, offs, out):
@@ -42,7 +47,7 @@ def tile_picked_place_lin_gelu_srt_l_kernel(tc, xT, w, b, gate, offs, out):
         grouped = [keep.tile([P, CHUNK * PACK], BF16, name="grouped%d" % c, align_bytes=64) for c in range(CHUNKS)]
         codes = [keep.tile([P, CHUNK], U32, name="codes%d" % c, align_bytes=64) for c in range(CHUNKS)]
         scales = [keep.tile([P, CHUNK], U8, name="scales%d" % c, align_bytes=64) for c in range(CHUNKS)]
-        gates = keep.tile([P, 3 * CHUNK], F32, name="gates")
+        gates = keep.tile([P, GATE_SLOTS * CHUNK], F32, name="gates")
         w_raw = keep.tile([P, PACK, N], F32, name="w_raw")
         w_grouped = keep.tile([P, N * PACK], BF16, name="w_grouped", align_bytes=64)
         w_codes = keep.tile([P, N], U32, name="w_codes", align_bytes=64)
@@ -59,7 +64,7 @@ def tile_picked_place_lin_gelu_srt_l_kernel(tc, xT, w, b, gate, offs, out):
             nc.sync.dma_start(raw[c, a][:], x_hbm[:, :, first : first + n])
 
         def gate_of(c, n=CHUNK):
-            a = (c + 1) % 3 * CHUNK
+            a = (c + 1) % GATE_SLOTS * CHUNK
             return gates[:, a : a + n]
 
         def load_gate(c):
@@ -74,9 +79,9 @@ def tile_picked_place_lin_gelu_srt_l_kernel(tc, xT, w, b, gate, offs, out):
         load_gate(1)
         load_x(2, 0, GROUP)
         load_x(2, GROUP, GROUP)
+        load_x(3, 0, CUT_OF_3)
+        load_x(3, CUT_OF_3, CHUNK - CUT_OF_3)
         load_gate(2)
-        load_x(3, 0, GROUP)
-        load_x(3, GROUP, GROUP)
 
         strip = windows[0][:, 0:CHUNK]
 
@@ -89,7 +94,7 @@ def tile_picked_place_lin_gelu_srt_l_kernel(tc, xT, w, b, gate, offs, out):
             target = dst[:, PACK * a : PACK * (a + n)].rearrange("p (c i t) -> p c t i", i=RUN, t=PACK)
             copy(out=target, in_=source)
 
-        def weave(copy, c, at, a, n):
+        def interleave_x(copy, c, at, a, n):
             interleave(copy, raw[c, at], grouped[c], at, a, n)
 
         def quantize(words, scale_bytes, src, a, n):
@@ -124,12 +129,9 @@ def tile_picked_place_lin_gelu_srt_l_kernel(tc, xT, w, b, gate, offs, out):
             a = c * CHUNK // STRIPE
             nc.vector.tensor_tensor(windows[k][:].indirect(offsets[:, a : a + n // STRIPE]), values, gate_of(c, n), MULT)
 
-        vals = {}
-
         def finish(c, k, firsts, tag=None):
             name = "values%d_%d" % (c, k)
             values = keep.tile([P, CHUNK], F32, name=name, tag=tag or name, align_bytes=64)
-            vals[c, k] = values
             n = CHUNK // len(firsts)
             for a in firsts:
                 activate(c, k, values[:, a : a + n], a, n)
@@ -143,25 +145,26 @@ def tile_picked_place_lin_gelu_srt_l_kernel(tc, xT, w, b, gate, offs, out):
 
         nc.vector.memset(strip, 0.0)
         clear(0, 1)
-        nc.scalar.activation(out=windows[1][:, 0:HALF], in_=windows[0][:, 0:HALF], func=GELU)
+        cleared = slice(0, SCALAR_CLEARS * CHUNK)
+        nc.scalar.activation(out=windows[1][:, cleared], in_=windows[0][:, cleared], func=GELU)
         interleave(on_scalar, w_raw, w_grouped, 0, 0, N)
         quantize(w_codes, w_scales, w_grouped, 0, N)
 
-        weave(on_vector, 0, 0, 0, GROUP)
-        weave(on_scalar, 0, 0, GROUP, GROUP)
+        interleave_x(on_vector, 0, 0, 0, GROUP)
+        interleave_x(on_scalar, 0, 0, GROUP, GROUP)
         for a in halves:
             quantize_x(0, a)
-        product(0, 1, 0)
-        product(0, 0, 1)
-        weave(on_vector, 1, 0, 0, GROUP)
+        product(0, 1, bank=0)
+        product(0, 0, bank=1)
+        interleave_x(on_vector, 1, 0, 0, GROUP)
         quantize_x(1, 0)
-        product(1, 0, 2, 0, GROUP)
-        weave(on_vector, 1, 0, GROUP, GROUP // 2)
-        weave(on_scalar, 1, 0, GROUP + GROUP // 2, GROUP // 2)
+        product(1, 0, bank=2, a=0, n=GROUP)
+        interleave_x(on_vector, 1, 0, GROUP, GROUP - SCALAR_OF_1)
+        interleave_x(on_scalar, 1, 0, CHUNK - SCALAR_OF_1, SCALAR_OF_1)
         quantize_x(1, GROUP)
-        product(1, 0, 3, GROUP, GROUP)
-        product(1, 1, 4)
-        clear(1, 2)
+        product(1, 0, bank=3, a=GROUP, n=GROUP)
+        product(1, 1, bank=4)
+        clear(1, SCALAR_CLEARS)
 
         finish(0, 1, whole)
         first_values = keep.tile([P, 2 * CHUNK], F32, name="first_values")
@@ -172,22 +175,23 @@ def tile_picked_place_lin_gelu_srt_l_kernel(tc, xT, w, b, gate, offs, out):
         store(0, 0, HALF)
         load_gate(3)
         for a in halves:
-            weave(on_scalar, 2, a, a, GROUP)
+            interleave_x(on_scalar, 2, a, a, GROUP)
             quantize_x(2, a)
-        product(2, 0, 5)
-        finish(1, 1, whole, tag="raw2_256")
+        product(2, 0, bank=5)
+        finish(1, 1, whole, tag="raw2_%d" % GROUP)
         store(1, 0, HALF)
 
-        weave(on_vector, 3, 0, 0, GROUP // 4)
-        weave(on_scalar, 3, 0, GROUP // 4, 3 * GROUP // 4)
+        interleave_x(on_vector, 3, 0, 0, VECTOR_OF_3)
+        interleave_x(on_scalar, 3, 0, VECTOR_OF_3, CUT_OF_3 - VECTOR_OF_3)
+        interleave_x(on_scalar, 3, CUT_OF_3, CUT_OF_3, CHUNK - CUT_OF_3)
         quantize_x(3, 0)
-        weave(on_scalar, 3, GROUP, GROUP, GROUP)
+        product(3, 0, bank=6, a=0, n=GROUP)
         quantize_x(3, GROUP)
-        product(3, 0, 0)
-        product(3, 1, 1)
-        finish(2, 0, whole, tag="raw3_256")
-        finish(3, 0, whole)
-        product(2, 1, 0)
+        product(3, 0, bank=7, a=GROUP, n=GROUP)
+        product(3, 1, bank=1)
+        finish(2, 0, whole)
+        finish(3, 0, halves)
+        product(2, 1, bank=7)
         store(0, HALF, T)
         for c in (2, 3):
             activate(c, 1, last_values[:, (c - 2) * CHUNK : (c - 1) * CHUNK])

@@ -13,9 +13,10 @@ U16 = mybir.dt.uint16
 U8 = mybir.dt.uint8
 FP8X4 = mybir.dt.float8_e4m3fn_x4
 GELU = mybir.ActivationFunctionType.Gelu_apprx_tanh
-MULT = mybir.AluOpType.mult
+ALU = mybir.AluOpType
 
 P = 128
+QUAD = 32
 PACK = 4
 STRIPE = 16
 CHUNK = 512
@@ -25,11 +26,12 @@ BLOCKS = N // P
 HALF = S // 2
 RUN = 4
 BIAS_PITCH = 8
-GATE_SLOTS = 3
-SCALAR_OF_1 = 128
-VECTOR_OF_3 = 64
-CUT_OF_3 = 384
-SCALAR_CLEARS = 2
+GATE_RUN = HALF // P
+SCALAR_OF_0 = 96
+VECTOR_OF_3 = 96
+SCALAR_CLEARS = 1536
+LATE_CLEARS = 1408
+A, B = 0, 1
 
 
 def tile_picked_place_lin_gelu_srt_l_kernel(tc, xT, w, b, gate, offs, out):
@@ -44,74 +46,97 @@ def tile_picked_place_lin_gelu_srt_l_kernel(tc, xT, w, b, gate, offs, out):
         x_hbm = xT.rearrange("(p t) s -> p t s", t=PACK)
         w_hbm = w.rearrange("(p t) m -> p t m", t=PACK)
 
-        grouped = [keep.tile([P, CHUNK * PACK], BF16, name="grouped%d" % c, align_bytes=64) for c in range(CHUNKS)]
+        windows = [keep.tile([P, T], F32, name="window%d" % k, align_bytes=64) for k in range(BLOCKS)]
+        grouped = {}
+        for c in range(CHUNKS):
+            for a in (0, GROUP):
+                grouped[c, a] = keep.tile([P, GROUP * PACK], BF16, name="grouped%d_%d" % (c, a), align_bytes=64)[:]
         codes = [keep.tile([P, CHUNK], U32, name="codes%d" % c, align_bytes=64) for c in range(CHUNKS)]
         scales = [keep.tile([P, CHUNK], U8, name="scales%d" % c, align_bytes=64) for c in range(CHUNKS)]
-        gates = keep.tile([P, GATE_SLOTS * CHUNK], F32, name="gates")
+        gate_row = keep.tile([P, 2, GATE_RUN], F32, name="gate_row")
+        gates = [keep.tile([P, HALF], F32, name="gates%d" % h) for h in range(2)]
         w_raw = keep.tile([P, PACK, N], F32, name="w_raw")
         w_grouped = keep.tile([P, N * PACK], BF16, name="w_grouped", align_bytes=64)
         w_codes = keep.tile([P, N], U32, name="w_codes", align_bytes=64)
         w_scales = keep.tile([P, N], U8, name="w_scales", align_bytes=64)
         bias = keep.tile([P, BLOCKS, BIAS_PITCH], F32, name="bias")
-        windows = [keep.tile([P, T], F32, name="window%d" % k) for k in range(BLOCKS)]
-        last_values = keep.tile([P, 2 * CHUNK], F32, name="last_values")
 
         raw = {}
 
+        first_a = keep.tile([P, GROUP + PACK * GROUP], F32, name="first_a", align_bytes=64)
+
         def load_x(c, a, n):
-            raw[c, a] = keep.tile([P, PACK, n], F32, name="raw%d_%d" % (c, a), align_bytes=64)
+            if (c, a) == (1, GROUP):
+                raw[c, a] = first_a[:, GROUP:].rearrange("p (t s) -> p t s", t=PACK)
+            elif (c, a) == (1, 0):
+                raw[c, a] = windows[A][:, T - PACK * n : T].rearrange("p (t s) -> p t s", t=PACK)
+            else:
+                raw[c, a] = keep.tile([P, PACK, n], F32, name="raw%d_%d" % (c, a), align_bytes=64)[:]
             first = c * CHUNK + a
-            nc.sync.dma_start(raw[c, a][:], x_hbm[:, :, first : first + n])
+            nc.sync.dma_start(raw[c, a], x_hbm[:, :, first : first + n])
 
-        def gate_of(c, n=CHUNK):
-            a = (c + 1) % GATE_SLOTS * CHUNK
-            return gates[:, a : a + n]
-
-        def load_gate(c):
-            nc.sync.dma_start(gate_of(c), gate[0:P, c * CHUNK : (c + 1) * CHUNK])
-
+        nc.sync.dma_start(gate_row[:], gate[0:1, :].rearrange("o (h p i) -> p (o h) i", h=2, p=P))
         nc.sync.dma_start(w_raw[:], w_hbm)
-        load_x(0, 0, CHUNK)
-        load_x(1, 0, CHUNK)
+        load_x(0, 0, GROUP)
+        load_x(0, GROUP, GROUP)
         nc.sync.dma_start(bias[:, :, 0:1], b.rearrange("(k p) o -> p k o", p=P))
-        load_gate(0)
+        load_x(1, 0, GROUP)
         nc.sync.dma_start(offsets[:], offs)
-        load_gate(1)
-        load_x(2, 0, GROUP)
-        load_x(2, GROUP, GROUP)
-        load_x(3, 0, CUT_OF_3)
-        load_x(3, CUT_OF_3, CHUNK - CUT_OF_3)
-        load_gate(2)
+        load_x(1, GROUP, GROUP)
+        load_x(2, 0, CHUNK)
+        load_x(3, 0, CHUNK)
 
-        strip = windows[0][:, 0:CHUNK]
+        def bank(number, name):
+            return psum.tile([P, CHUNK], F32, name=name, tag="bank%d" % number)
 
-        def clear(k, first):
-            for q in range(first, T // CHUNK):
-                nc.vector.tensor_copy(out=windows[k][:, q * CHUNK : (q + 1) * CHUNK], in_=strip)
+        ones = keep.tile([P, P], F32, name="ones")
+        quad_start = keep.tile([P, 1], F32, name="quad_start")
+        counts = keep.tile([P, P], F32, name="counts", align_bytes=64)
+        lanes = keep.tile([P, QUAD], F32, name="lanes", align_bytes=64)
+        identity = keep.tile([P, P], F32, name="identity")
+        nc.gpsimd.memset(ones[:], 1.0)
+        for q in range(0, P, QUAD):
+            nc.gpsimd.memset(quad_start[q : q + QUAD, :], float(q))
+        nc.vector.tensor_tensor_scan(counts[:], ones[:], ones[:], 0.0, ALU.mult, ALU.add)
+        nc.vector.transpose(lanes[:], counts[:, 0:QUAD])
+        nc.vector.tensor_scalar(identity[:], counts[:], quad_start[:, 0:1], lanes[:, 0:1], ALU.subtract, ALU.is_equal)
 
-        def interleave(copy, src, dst, at, a, n):
-            source = src[:, :, a - at : a - at + n].rearrange("p t (c i) -> p c t i", i=RUN)
-            target = dst[:, PACK * a : PACK * (a + n)].rearrange("p (c i t) -> p c t i", i=RUN, t=PACK)
-            copy(out=target, in_=source)
+        def clear(k, first, last):
+            for a in range(first, last, HALF):
+                n = min(HALF, last - a)
+                nc.vector.tensor_copy(out=windows[k][:, a : a + n], in_=windows[B][:, 0:n])
 
-        def interleave_x(copy, c, at, a, n):
-            interleave(copy, raw[c, at], grouped[c], at, a, n)
+        def spread_gate(copy, h, u, number):
+            spread = bank(number, "spread%d_%d" % (h, u))
+            for r in range(RUN):
+                i = RUN * u + r
+                column = gate_row[:, h, i : i + 1].to_broadcast([P, P])
+                nc.tensor.transpose(spread[:, r * P : (r + 1) * P], column, identity[:])
+            target = gates[h][:].rearrange("q (p u r) -> q u p r", u=GATE_RUN // RUN, r=RUN)
+            copy(out=target[:, u], in_=spread[:].rearrange("q (r p) -> q p r", r=RUN))
 
-        def quantize(words, scale_bytes, src, a, n):
-            nc.vector.quantize_mx(
-                out=words[:, a : a + n].bitcast(FP8X4),
-                scales=scale_bytes[:, a : a + n],
-                in_=src[:, PACK * a : PACK * (a + n)],
+        def interleave(copy, source, target):
+            copy(
+                out=target.rearrange("p (c i t) -> p c t i", i=RUN, t=PACK),
+                in_=source.rearrange("p t (c i) -> p c t i", i=RUN),
             )
 
+        def interleave_x(copy, c, at, a, n):
+            group = a // GROUP * GROUP
+            target = grouped[c, group][:, PACK * (a - group) : PACK * (a - group + n)]
+            interleave(copy, raw[c, at][:, :, a - at : a - at + n], target)
+
+        def quantize(words, scale_bytes, source):
+            nc.vector.quantize_mx(out=words.bitcast(FP8X4), scales=scale_bytes, in_=source)
+
         def quantize_x(c, a):
-            quantize(codes[c], scales[c], grouped[c], a, GROUP)
+            quantize(codes[c][:, a : a + GROUP], scales[c][:, a : a + GROUP], grouped[c, a])
 
         sums = {}
 
-        def product(c, k, bank, a=0, n=CHUNK):
+        def product(c, k, number, a=0, n=CHUNK):
             mine = slice(k * P, (k + 1) * P)
-            sums[c, k, a] = psum.tile([P, CHUNK], F32, name="sums%d_%d_%d" % (c, k, a), tag="bank%d" % bank)
+            sums[c, k, a] = bank(number, "sums%d_%d_%d" % (c, k, a))
             nc.tensor.matmul_mx(
                 out=sums[c, k, a][:, 0:n],
                 lhsT=w_codes[:, mine].bitcast(FP8X4),
@@ -122,78 +147,93 @@ def tile_picked_place_lin_gelu_srt_l_kernel(tc, xT, w, b, gate, offs, out):
                 stop=True,
             )
 
-        def activate(c, k, target, a=0, n=CHUNK):
-            nc.scalar.activation(out=target, in_=sums[c, k, a][:, 0:n], func=GELU, bias=bias[:, k, 0:1])
-
-        def place(c, k, values, n=CHUNK):
-            a = c * CHUNK // STRIPE
-            nc.vector.tensor_tensor(windows[k][:].indirect(offsets[:, a : a + n // STRIPE]), values, gate_of(c, n), MULT)
-
-        def finish(c, k, firsts, tag=None):
-            name = "values%d_%d" % (c, k)
-            values = keep.tile([P, CHUNK], F32, name=name, tag=tag or name, align_bytes=64)
+        def activate(c, k, values, firsts):
             n = CHUNK // len(firsts)
             for a in firsts:
-                activate(c, k, values[:, a : a + n], a, n)
-            place(c, k, values[:])
+                nc.scalar.activation(
+                    out=values[:, a : a + n], in_=sums[c, k, a][:, 0:n], func=GELU, bias=bias[:, k, 0:1]
+                )
+
+        def place(c, k, values, n=CHUNK):
+            a = c * CHUNK
+            weights = gates[a // HALF][:, a % HALF : a % HALF + n]
+            where = offsets[:, a // STRIPE : (a + n) // STRIPE]
+            nc.vector.tensor_tensor(windows[k][:].indirect(where), values, weights, ALU.mult)
 
         def store(k, c0, c1):
             nc.sync.dma_start(out[k * P : (k + 1) * P, c0:c1], windows[k][:, c0:c1])
 
+        def pair(name, tag=None):
+            both = keep.tile([P, 2 * CHUNK], F32, name=name, tag=tag or name, align_bytes=64)
+            return both, both[:, 0:CHUNK], both[:, CHUNK : 2 * CHUNK]
+
         on_vector, on_scalar = nc.vector.tensor_copy, nc.scalar.copy
         halves, whole = (0, GROUP), (0,)
 
-        nc.vector.memset(strip, 0.0)
-        clear(0, 1)
-        cleared = slice(0, SCALAR_CLEARS * CHUNK)
-        nc.scalar.activation(out=windows[1][:, cleared], in_=windows[0][:, cleared], func=GELU)
-        interleave(on_scalar, w_raw, w_grouped, 0, 0, N)
-        quantize(w_codes, w_scales, w_grouped, 0, N)
+        nc.vector.memset(windows[B][:, 0:CHUNK], 0.0)
+        clear(B, CHUNK, HALF)
+        clear(B, HALF, T)
+        clear(A, SCALAR_CLEARS, T - LATE_CLEARS)
+        zeros = windows[B][:, 0:CHUNK].unsqueeze(1).to_broadcast([P, SCALAR_CLEARS // CHUNK, CHUNK])
+        cleared = windows[A][:, 0:SCALAR_CLEARS].rearrange("p (n s) -> p n s", s=CHUNK)
+        nc.scalar.activation(out=cleared, in_=zeros, func=GELU)
+        interleave(on_vector, w_raw[:], w_grouped[:])
+        quantize(w_codes[:], w_scales[:], w_grouped[:])
+        for number in range(4):
+            spread_gate(on_scalar, number // 2, number % 2, number)
 
         interleave_x(on_vector, 0, 0, 0, GROUP)
-        interleave_x(on_scalar, 0, 0, GROUP, GROUP)
-        for a in halves:
-            quantize_x(0, a)
-        product(0, 1, bank=0)
-        product(0, 0, bank=1)
+        quantize_x(0, 0)
+        product(0, B, 4, 0, GROUP)
+        product(0, A, 6, 0, GROUP)
+        interleave_x(on_vector, 0, GROUP, GROUP, GROUP - SCALAR_OF_0)
+        interleave_x(on_scalar, 0, GROUP, CHUNK - SCALAR_OF_0, SCALAR_OF_0)
+        quantize_x(0, GROUP)
+        product(0, B, 5, GROUP, GROUP)
+        product(0, A, 7, GROUP, GROUP)
+        values0_b = keep.tile([P, CHUNK], F32, name="values0_b")
+        values0_a, values1_a = first_a[:, 0:CHUNK], first_a[:, CHUNK : 2 * CHUNK]
+        activate(0, B, values0_b[:], halves)
         interleave_x(on_vector, 1, 0, 0, GROUP)
+        nc.gpsimd.memset(windows[A][:, T - LATE_CLEARS : T], 0.0)
+        place(0, B, values0_b[:])
         quantize_x(1, 0)
-        product(1, 0, bank=2, a=0, n=GROUP)
-        interleave_x(on_vector, 1, 0, GROUP, GROUP - SCALAR_OF_1)
-        interleave_x(on_scalar, 1, 0, CHUNK - SCALAR_OF_1, SCALAR_OF_1)
+        product(1, A, 0, 0, GROUP)
+        interleave_x(on_scalar, 1, GROUP, GROUP, GROUP)
         quantize_x(1, GROUP)
-        product(1, 0, bank=3, a=GROUP, n=GROUP)
-        product(1, 1, bank=4)
-        clear(1, SCALAR_CLEARS)
+        product(1, A, 2, GROUP, GROUP)
+        product(1, B, 3)
+        activate(0, A, values0_a, halves)
+        place(0, A, values0_a)
+        activate(1, A, values1_a, halves)
+        place(1, A, values1_a)
+        store(A, 0, HALF)
 
-        finish(0, 1, whole)
-        first_values = keep.tile([P, 2 * CHUNK], F32, name="first_values")
-        activate(0, 0, first_values[:, 0:CHUNK])
         for a in halves:
-            activate(1, 0, first_values[:, CHUNK + a : CHUNK + a + GROUP], a, GROUP)
-        place(0, 0, first_values[:], 2 * CHUNK)
-        store(0, 0, HALF)
-        load_gate(3)
-        for a in halves:
-            interleave_x(on_scalar, 2, a, a, GROUP)
+            interleave_x(on_scalar, 2, 0, a, GROUP)
             quantize_x(2, a)
-        product(2, 0, bank=5)
-        finish(1, 1, whole, tag="raw2_%d" % GROUP)
-        store(1, 0, HALF)
+        product(2, A, 4)
+        values1_b = keep.tile([P, CHUNK], F32, name="values1_b", tag="raw2_0", align_bytes=64)
+        activate(1, B, values1_b[:], whole)
+        place(1, B, values1_b[:])
+        store(B, 0, HALF)
 
         interleave_x(on_vector, 3, 0, 0, VECTOR_OF_3)
-        interleave_x(on_scalar, 3, 0, VECTOR_OF_3, CUT_OF_3 - VECTOR_OF_3)
-        interleave_x(on_scalar, 3, CUT_OF_3, CUT_OF_3, CHUNK - CUT_OF_3)
-        quantize_x(3, 0)
-        product(3, 0, bank=6, a=0, n=GROUP)
-        quantize_x(3, GROUP)
-        product(3, 0, bank=7, a=GROUP, n=GROUP)
-        product(3, 1, bank=1)
-        finish(2, 0, whole)
-        finish(3, 0, halves)
-        product(2, 1, bank=7)
-        store(0, HALF, T)
-        for c in (2, 3):
-            activate(c, 1, last_values[:, (c - 2) * CHUNK : (c - 1) * CHUNK])
-        place(2, 1, last_values[:], 2 * CHUNK)
-        store(1, HALF, T)
+        interleave_x(on_scalar, 3, 0, GROUP, GROUP)
+        interleave_x(on_scalar, 3, 0, VECTOR_OF_3, GROUP - VECTOR_OF_3)
+        for a in reversed(halves):
+            quantize_x(3, a)
+            product(3, A, 5 + a // GROUP, a, GROUP)
+        product(3, B, 7)
+        values_a, values2_a, values3_a = pair("values_a", tag="raw3_0")
+        activate(2, A, values2_a, whole)
+        place(2, A, values2_a)
+        activate(3, A, values3_a, halves)
+        place(3, A, values3_a)
+        product(2, B, 6)
+        store(A, HALF, T)
+        values_b, values2_b, values3_b = pair("values_b")
+        activate(2, B, values2_b, whole)
+        activate(3, B, values3_b, whole)
+        place(2, B, values_b[:], 2 * CHUNK)
+        store(B, HALF, T)

@@ -25,6 +25,7 @@ GROUP = CHUNK // 2
 BLOCKS = N // P
 HALF = S // 2
 RUN = 4
+SCALAR_RUN = 2
 BIAS_PITCH = 8
 GATE_RUN = HALF // P
 SCALAR_OF_0 = 96
@@ -116,9 +117,10 @@ def tile_picked_place_lin_gelu_srt_l_kernel(tc, xT, w, b, gate, offs, out):
             copy(out=target[:, u], in_=spread[:].rearrange("q (r p) -> q p r", r=RUN))
 
         def interleave(copy, source, target):
-            copy(
-                out=target.rearrange("p (c i t) -> p c t i", i=RUN, t=PACK),
-                in_=source.rearrange("p t (c i) -> p c t i", i=RUN),
+            engine, run = copy
+            engine(
+                out=target.rearrange("p (c i t) -> p c t i", i=run, t=PACK),
+                in_=source.rearrange("p t (c i) -> p c t i", i=run),
             )
 
         def interleave_x(copy, c, at, a, n):
@@ -167,7 +169,7 @@ def tile_picked_place_lin_gelu_srt_l_kernel(tc, xT, w, b, gate, offs, out):
             both = keep.tile([P, 2 * CHUNK], F32, name=name, tag=tag or name, align_bytes=64)
             return both, both[:, 0:CHUNK], both[:, CHUNK : 2 * CHUNK]
 
-        on_vector, on_scalar = nc.vector.tensor_copy, nc.scalar.copy
+        on_vector, on_scalar = (nc.vector.tensor_copy, RUN), (nc.scalar.copy, SCALAR_RUN)
         halves, whole = (0, GROUP), (0,)
 
         nc.vector.memset(windows[B][:, 0:CHUNK], 0.0)
@@ -180,7 +182,7 @@ def tile_picked_place_lin_gelu_srt_l_kernel(tc, xT, w, b, gate, offs, out):
         interleave(on_vector, w_raw[:], w_grouped[:])
         quantize(w_codes[:], w_scales[:], w_grouped[:])
         for number in range(4):
-            spread_gate(on_scalar, number // 2, number % 2, number)
+            spread_gate(nc.scalar.copy, number // 2, number % 2, number)
 
         interleave_x(on_vector, 0, 0, 0, GROUP)
         quantize_x(0, 0)

@@ -28,10 +28,11 @@ RUN = 4
 SCALAR_RUN = 2
 BIAS_PITCH = 8
 GATE_RUN = HALF // P
-SCALAR_OF_0 = 96
-VECTOR_OF_3 = 96
-SCALAR_CLEARS = 1536
-LATE_CLEARS = 1408
+SCALAR_OF_0 = 192
+CUT_OF_1 = 320
+VECTOR_OF_3 = 64
+LENT = 64
+SCALAR_CLEARS = 1024
 A, B = 0, 1
 
 
@@ -48,13 +49,10 @@ def tile_picked_place_lin_gelu_srt_l_kernel(tc, xT, w, b, gate, offs, out):
         w_hbm = w.rearrange("(p t) m -> p t m", t=PACK)
 
         windows = [keep.tile([P, T], F32, name="window%d" % k, align_bytes=64) for k in range(BLOCKS)]
-        grouped = {}
-        for c in range(CHUNKS):
-            for a in (0, GROUP):
-                grouped[c, a] = keep.tile([P, GROUP * PACK], BF16, name="grouped%d_%d" % (c, a), align_bytes=64)[:]
+        grouped = [keep.tile([P, CHUNK * PACK], BF16, name="grouped%d" % c, align_bytes=64) for c in range(CHUNKS)]
         codes = [keep.tile([P, CHUNK], U32, name="codes%d" % c, align_bytes=64) for c in range(CHUNKS)]
         scales = [keep.tile([P, CHUNK], U8, name="scales%d" % c, align_bytes=64) for c in range(CHUNKS)]
-        gate_row = keep.tile([P, 2, GATE_RUN], F32, name="gate_row")
+        gate_row = keep.tile([P, GATE_RUN], F32, name="gate_row")
         gates = [keep.tile([P, HALF], F32, name="gates%d" % h) for h in range(2)]
         w_raw = keep.tile([P, PACK, N], F32, name="w_raw")
         w_grouped = keep.tile([P, N * PACK], BF16, name="w_grouped", align_bytes=64)
@@ -64,28 +62,32 @@ def tile_picked_place_lin_gelu_srt_l_kernel(tc, xT, w, b, gate, offs, out):
 
         raw = {}
 
-        first_a = keep.tile([P, GROUP + PACK * GROUP], F32, name="first_a", align_bytes=64)
+        def lend(name, lent, n):
+            both = keep.tile([P, CHUNK - lent + PACK * n], F32, name=name, align_bytes=64)
+            return both[:, 0:CHUNK], both[:, CHUNK - lent :].rearrange("p (t s) -> p t s", t=PACK)
+
+        values0_b, raw[1, CUT_OF_1] = lend("values0_b", LENT, CHUNK - CUT_OF_1)
+        values1_a, raw[2, 0] = lend("values1_a", LENT, GROUP)
+        values1_b, raw[2, GROUP] = lend("values1_b", LENT, GROUP)
+        values2_a, raw[3, 0] = lend("values2_a", GROUP + LENT, CHUNK)
 
         def load_x(c, a, n):
-            if (c, a) == (1, GROUP):
-                raw[c, a] = first_a[:, GROUP:].rearrange("p (t s) -> p t s", t=PACK)
-            elif (c, a) == (1, 0):
-                raw[c, a] = windows[A][:, T - PACK * n : T].rearrange("p (t s) -> p t s", t=PACK)
-            else:
+            if (c, a) not in raw:
                 raw[c, a] = keep.tile([P, PACK, n], F32, name="raw%d_%d" % (c, a), align_bytes=64)[:]
             first = c * CHUNK + a
             nc.sync.dma_start(raw[c, a], x_hbm[:, :, first : first + n])
 
-        nc.sync.dma_start(gate_row[:], gate[0:1, :].rearrange("o (h p i) -> p (o h) i", h=2, p=P))
+        nc.sync.dma_start(gate_row[:], gate[0:1, 0:HALF].rearrange("o (p i) -> p (o i)", p=P))
         nc.sync.dma_start(w_raw[:], w_hbm)
-        load_x(0, 0, GROUP)
-        load_x(0, GROUP, GROUP)
+        load_x(0, 0, CHUNK)
         nc.sync.dma_start(bias[:, :, 0:1], b.rearrange("(k p) o -> p k o", p=P))
-        load_x(1, 0, GROUP)
+        load_x(1, 0, CUT_OF_1)
         nc.sync.dma_start(offsets[:], offs)
-        load_x(1, GROUP, GROUP)
-        load_x(2, 0, CHUNK)
+        load_x(1, CUT_OF_1, CHUNK - CUT_OF_1)
+        load_x(2, 0, GROUP)
+        load_x(2, GROUP, GROUP)
         load_x(3, 0, CHUNK)
+        nc.sync.dma_start(gates[1][:], gate[0:P, HALF:S])
 
         def bank(number, name):
             return psum.tile([P, CHUNK], F32, name=name, tag="bank%d" % number)
@@ -105,16 +107,16 @@ def tile_picked_place_lin_gelu_srt_l_kernel(tc, xT, w, b, gate, offs, out):
         def clear(k, first, last):
             for a in range(first, last, HALF):
                 n = min(HALF, last - a)
-                nc.vector.tensor_copy(out=windows[k][:, a : a + n], in_=windows[B][:, 0:n])
+                nc.vector.tensor_copy(out=windows[k][:, a : a + n], in_=windows[A][:, 0:n])
 
-        def spread_gate(copy, h, u, number):
-            spread = bank(number, "spread%d_%d" % (h, u))
+        def spread_gate(u):
+            spread = bank(u, "spread%d" % u)
             for r in range(RUN):
                 i = RUN * u + r
-                column = gate_row[:, h, i : i + 1].to_broadcast([P, P])
+                column = gate_row[:, i : i + 1].to_broadcast([P, P])
                 nc.tensor.transpose(spread[:, r * P : (r + 1) * P], column, identity[:])
-            target = gates[h][:].rearrange("q (p u r) -> q u p r", u=GATE_RUN // RUN, r=RUN)
-            copy(out=target[:, u], in_=spread[:].rearrange("q (r p) -> q p r", r=RUN))
+            target = gates[0][:].rearrange("q (p u r) -> q u p r", u=GATE_RUN // RUN, r=RUN)
+            nc.scalar.copy(out=target[:, u], in_=spread[:].rearrange("q (r p) -> q p r", r=RUN))
 
         def interleave(copy, source, target):
             engine, run = copy
@@ -124,15 +126,13 @@ def tile_picked_place_lin_gelu_srt_l_kernel(tc, xT, w, b, gate, offs, out):
             )
 
         def interleave_x(copy, c, at, a, n):
-            group = a // GROUP * GROUP
-            target = grouped[c, group][:, PACK * (a - group) : PACK * (a - group + n)]
-            interleave(copy, raw[c, at][:, :, a - at : a - at + n], target)
+            interleave(copy, raw[c, at][:, :, a - at : a - at + n], grouped[c][:, PACK * a : PACK * (a + n)])
 
         def quantize(words, scale_bytes, source):
             nc.vector.quantize_mx(out=words.bitcast(FP8X4), scales=scale_bytes, in_=source)
 
-        def quantize_x(c, a):
-            quantize(codes[c][:, a : a + GROUP], scales[c][:, a : a + GROUP], grouped[c, a])
+        def quantize_x(c, a=0, n=CHUNK):
+            quantize(codes[c][:, a : a + n], scales[c][:, a : a + n], grouped[c][:, PACK * a : PACK * (a + n)])
 
         sums = {}
 
@@ -149,12 +149,10 @@ def tile_picked_place_lin_gelu_srt_l_kernel(tc, xT, w, b, gate, offs, out):
                 stop=True,
             )
 
-        def activate(c, k, values, firsts):
-            n = CHUNK // len(firsts)
-            for a in firsts:
-                nc.scalar.activation(
-                    out=values[:, a : a + n], in_=sums[c, k, a][:, 0:n], func=GELU, bias=bias[:, k, 0:1]
-                )
+        def activate(c, k, values, a=0, n=CHUNK, at=None):
+            at = a if at is None else at
+            source = sums[c, k, at][:, a - at : a - at + n]
+            nc.scalar.activation(out=values[:, a : a + n], in_=source, func=GELU, bias=bias[:, k, 0:1])
 
         def place(c, k, values, n=CHUNK):
             a = c * CHUNK
@@ -165,77 +163,71 @@ def tile_picked_place_lin_gelu_srt_l_kernel(tc, xT, w, b, gate, offs, out):
         def store(k, c0, c1):
             nc.sync.dma_start(out[k * P : (k + 1) * P, c0:c1], windows[k][:, c0:c1])
 
-        def pair(name, tag=None):
-            both = keep.tile([P, 2 * CHUNK], F32, name=name, tag=tag or name, align_bytes=64)
-            return both, both[:, 0:CHUNK], both[:, CHUNK : 2 * CHUNK]
-
         on_vector, on_scalar = (nc.vector.tensor_copy, RUN), (nc.scalar.copy, SCALAR_RUN)
-        halves, whole = (0, GROUP), (0,)
+        halves = (0, GROUP)
 
-        nc.vector.memset(windows[B][:, 0:CHUNK], 0.0)
-        clear(B, CHUNK, HALF)
-        clear(B, HALF, T)
-        clear(A, SCALAR_CLEARS, T - LATE_CLEARS)
-        zeros = windows[B][:, 0:CHUNK].unsqueeze(1).to_broadcast([P, SCALAR_CLEARS // CHUNK, CHUNK])
-        cleared = windows[A][:, 0:SCALAR_CLEARS].rearrange("p (n s) -> p n s", s=CHUNK)
+        nc.vector.memset(windows[A][:, 0:CHUNK], 0.0)
+        clear(A, CHUNK, HALF)
+        clear(A, HALF, T)
+        clear(B, SCALAR_CLEARS, T)
+        zeros = windows[A][:, 0:CHUNK].unsqueeze(1).to_broadcast([P, SCALAR_CLEARS // CHUNK, CHUNK])
+        cleared = windows[B][:, 0:SCALAR_CLEARS].rearrange("p (n s) -> p n s", s=CHUNK)
         nc.scalar.activation(out=cleared, in_=zeros, func=GELU)
-        interleave(on_vector, w_raw[:], w_grouped[:])
+        interleave(on_scalar, w_raw[:], w_grouped[:])
         quantize(w_codes[:], w_scales[:], w_grouped[:])
-        for number in range(4):
-            spread_gate(nc.scalar.copy, number // 2, number % 2, number)
+        spread_gate(0)
+
+        def in_two(c, at, a, n):
+            interleave_x(on_scalar, c, at, a, n // 2)
+            interleave_x(on_scalar, c, at, a + n // 2, n // 2)
 
         interleave_x(on_vector, 0, 0, 0, GROUP)
-        quantize_x(0, 0)
-        product(0, B, 4, 0, GROUP)
-        product(0, A, 6, 0, GROUP)
-        interleave_x(on_vector, 0, GROUP, GROUP, GROUP - SCALAR_OF_0)
-        interleave_x(on_scalar, 0, GROUP, CHUNK - SCALAR_OF_0, SCALAR_OF_0)
-        quantize_x(0, GROUP)
-        product(0, B, 5, GROUP, GROUP)
-        product(0, A, 7, GROUP, GROUP)
-        values0_b = keep.tile([P, CHUNK], F32, name="values0_b")
-        values0_a, values1_a = first_a[:, 0:CHUNK], first_a[:, CHUNK : 2 * CHUNK]
-        activate(0, B, values0_b[:], halves)
-        interleave_x(on_vector, 1, 0, 0, GROUP)
-        nc.gpsimd.memset(windows[A][:, T - LATE_CLEARS : T], 0.0)
-        place(0, B, values0_b[:])
-        quantize_x(1, 0)
-        product(1, A, 0, 0, GROUP)
-        interleave_x(on_scalar, 1, GROUP, GROUP, GROUP)
-        quantize_x(1, GROUP)
-        product(1, A, 2, GROUP, GROUP)
-        product(1, B, 3)
-        activate(0, A, values0_a, halves)
-        place(0, A, values0_a)
-        activate(1, A, values1_a, halves)
+        interleave_x(on_vector, 0, 0, GROUP, GROUP - SCALAR_OF_0)
+        interleave_x(on_scalar, 0, 0, CHUNK - SCALAR_OF_0, SCALAR_OF_0)
+        spread_gate(1)
+        values0_a = keep.tile([P, CHUNK], F32, name="values0_a")
+        for a in halves:
+            quantize_x(0, a, GROUP)
+            product(0, A, 2 + a // GROUP, a, GROUP)
+            activate(0, A, values0_a, a, GROUP)
+        product(0, B, 4)
+        activate(0, B, values0_b, 0, GROUP)
+        interleave_x(on_vector, 1, 0, 0, CUT_OF_1)
+        place(0, A, values0_a[:])
+        in_two(1, CUT_OF_1, CUT_OF_1, CHUNK - CUT_OF_1)
+        quantize_x(1)
+        product(1, A, 5)
+        product(1, B, 6)
+        activate(0, B, values0_b, GROUP, GROUP, at=0)
+        place(0, B, values0_b)
+        in_two(2, 0, 0, GROUP)
+        activate(1, A, values1_a)
         place(1, A, values1_a)
         store(A, 0, HALF)
-
-        for a in halves:
-            interleave_x(on_scalar, 2, 0, a, GROUP)
-            quantize_x(2, a)
-        product(2, A, 4)
-        values1_b = keep.tile([P, CHUNK], F32, name="values1_b", tag="raw2_0", align_bytes=64)
-        activate(1, B, values1_b[:], whole)
-        place(1, B, values1_b[:])
+        in_two(2, GROUP, GROUP, GROUP)
+        quantize_x(2)
+        product(2, A, 7)
+        activate(1, B, values1_b)
+        place(1, B, values1_b)
         store(B, 0, HALF)
 
-        interleave_x(on_vector, 3, 0, 0, VECTOR_OF_3)
-        interleave_x(on_scalar, 3, 0, GROUP, GROUP)
-        interleave_x(on_scalar, 3, 0, VECTOR_OF_3, GROUP - VECTOR_OF_3)
-        for a in reversed(halves):
-            quantize_x(3, a)
-            product(3, A, 5 + a // GROUP, a, GROUP)
-        product(3, B, 7)
-        values_a, values2_a, values3_a = pair("values_a", tag="raw3_0")
-        activate(2, A, values2_a, whole)
+        interleave_x(on_vector, 3, 0, CHUNK - VECTOR_OF_3, VECTOR_OF_3)
+        interleave_x(on_scalar, 3, 0, 0, GROUP)
+        in_two(3, 0, GROUP, GROUP - VECTOR_OF_3)
+        for a in halves:
+            quantize_x(3, a, GROUP)
+            product(3, A, a // GROUP, a, GROUP)
+        product(3, B, 2)
+        activate(2, A, values2_a)
         place(2, A, values2_a)
-        activate(3, A, values3_a, halves)
-        place(3, A, values3_a)
-        product(2, B, 6)
+        values3_a = keep.tile([P, CHUNK], F32, name="values3_a")
+        for a in halves:
+            activate(3, A, values3_a, a, GROUP)
+        place(3, A, values3_a[:])
+        product(2, B, 1)
         store(A, HALF, T)
-        values_b, values2_b, values3_b = pair("values_b")
-        activate(2, B, values2_b, whole)
-        activate(3, B, values3_b, whole)
-        place(2, B, values_b[:], 2 * CHUNK)
+        values_b = keep.tile([P, HALF], F32, name="values_b")
+        activate(2, B, values_b[:, 0:CHUNK])
+        activate(3, B, values_b[:, CHUNK:HALF])
+        place(2, B, values_b[:], HALF)
         store(B, HALF, T)

@@ -28,9 +28,9 @@ RUN = 4
 SCALAR_RUN = 2
 BIAS_PITCH = 8
 GATE_RUN = HALF // P
-SCALAR_OF_0 = 192
-CUT_OF_1 = 320
-VECTOR_OF_3 = 64
+SCALAR_OF_0 = 160
+CUT_OF_1 = 352
+VECTOR_OF_3 = 96
 LENT = 64
 SCALAR_CLEARS = 1024
 A, B = 0, 1
@@ -53,7 +53,7 @@ def tile_picked_place_lin_gelu_srt_l_kernel(tc, xT, w, b, gate, offs, out):
         codes = [keep.tile([P, CHUNK], U32, name="codes%d" % c, align_bytes=64) for c in range(CHUNKS)]
         scales = [keep.tile([P, CHUNK], U8, name="scales%d" % c, align_bytes=64) for c in range(CHUNKS)]
         gate_row = keep.tile([P, GATE_RUN], F32, name="gate_row")
-        gates = [keep.tile([P, HALF], F32, name="gates%d" % h) for h in range(2)]
+        spread_gates = keep.tile([P, HALF], F32, name="spread_gates")
         w_raw = keep.tile([P, PACK, N], F32, name="w_raw")
         w_grouped = keep.tile([P, N * PACK], BF16, name="w_grouped", align_bytes=64)
         w_codes = keep.tile([P, N], U32, name="w_codes", align_bytes=64)
@@ -62,12 +62,14 @@ def tile_picked_place_lin_gelu_srt_l_kernel(tc, xT, w, b, gate, offs, out):
 
         raw = {}
 
-        def lend(name, lent, n):
-            both = keep.tile([P, CHUNK - lent + PACK * n], F32, name=name, align_bytes=64)
-            return both[:, 0:CHUNK], both[:, CHUNK - lent :].rearrange("p (t s) -> p t s", t=PACK)
+        def lend(name, lent, n, lead=0):
+            end = lead + CHUNK
+            both = keep.tile([P, end - lent + PACK * n], F32, name=name, align_bytes=64)
+            return both[:, 0:end], both[:, end - lent :].rearrange("p (t s) -> p t s", t=PACK)
 
         values0_b, raw[1, CUT_OF_1] = lend("values0_b", LENT, CHUNK - CUT_OF_1)
-        values1_a, raw[2, 0] = lend("values1_a", LENT, GROUP)
+        late_gates, raw[2, 0] = lend("late_gates", LENT, GROUP, lead=CHUNK)
+        values1_a = late_gates[:, CHUNK:HALF]
         values1_b, raw[2, GROUP] = lend("values1_b", LENT, GROUP)
         values2_a, raw[3, 0] = lend("values2_a", GROUP + LENT, CHUNK)
 
@@ -80,14 +82,18 @@ def tile_picked_place_lin_gelu_srt_l_kernel(tc, xT, w, b, gate, offs, out):
         nc.sync.dma_start(gate_row[:], gate[0:1, 0:HALF].rearrange("o (p i) -> p (o i)", p=P))
         nc.sync.dma_start(w_raw[:], w_hbm)
         load_x(0, 0, CHUNK)
-        nc.sync.dma_start(bias[:, :, 0:1], b.rearrange("(k p) o -> p k o", p=P))
         load_x(1, 0, CUT_OF_1)
+        nc.sync.dma_start(bias[:, :, 0:1], b.rearrange("(k p) o -> p k o", p=P))
         nc.sync.dma_start(offsets[:], offs)
         load_x(1, CUT_OF_1, CHUNK - CUT_OF_1)
         load_x(2, 0, GROUP)
         load_x(2, GROUP, GROUP)
         load_x(3, 0, CHUNK)
-        nc.sync.dma_start(gates[1][:], gate[0:P, HALF:S])
+
+        def load_gate(c):
+            nc.sync.dma_start(late_gates[:, (c - 2) * CHUNK : (c - 1) * CHUNK], gate[0:P, c * CHUNK : (c + 1) * CHUNK])
+
+        load_gate(2)
 
         def bank(number, name):
             return psum.tile([P, CHUNK], F32, name=name, tag="bank%d" % number)
@@ -115,7 +121,7 @@ def tile_picked_place_lin_gelu_srt_l_kernel(tc, xT, w, b, gate, offs, out):
                 i = RUN * u + r
                 column = gate_row[:, i : i + 1].to_broadcast([P, P])
                 nc.tensor.transpose(spread[:, r * P : (r + 1) * P], column, identity[:])
-            target = gates[0][:].rearrange("q (p u r) -> q u p r", u=GATE_RUN // RUN, r=RUN)
+            target = spread_gates[:].rearrange("q (p u r) -> q u p r", u=GATE_RUN // RUN, r=RUN)
             nc.scalar.copy(out=target[:, u], in_=spread[:].rearrange("q (r p) -> q p r", r=RUN))
 
         def interleave(copy, source, target):
@@ -138,9 +144,13 @@ def tile_picked_place_lin_gelu_srt_l_kernel(tc, xT, w, b, gate, offs, out):
 
         def product(c, k, number, a=0, n=CHUNK):
             mine = slice(k * P, (k + 1) * P)
-            sums[c, k, a] = bank(number, "sums%d_%d_%d" % (c, k, a))
+            if number is None:
+                target = sums[c, k, 0][:, a : a + n]
+            else:
+                sums[c, k, a] = bank(number, "sums%d_%d_%d" % (c, k, a))
+                target = sums[c, k, a][:, 0:n]
             nc.tensor.matmul_mx(
-                out=sums[c, k, a][:, 0:n],
+                out=target,
                 lhsT=w_codes[:, mine].bitcast(FP8X4),
                 lhsT_scale=w_scales[:, mine],
                 rhs=codes[c][:, a : a + n].bitcast(FP8X4),
@@ -154,9 +164,8 @@ def tile_picked_place_lin_gelu_srt_l_kernel(tc, xT, w, b, gate, offs, out):
             source = sums[c, k, at][:, a - at : a - at + n]
             nc.scalar.activation(out=values[:, a : a + n], in_=source, func=GELU, bias=bias[:, k, 0:1])
 
-        def place(c, k, values, n=CHUNK):
-            a = c * CHUNK
-            weights = gates[a // HALF][:, a % HALF : a % HALF + n]
+        def place(c, k, values, weights):
+            a, n = c * CHUNK, values.shape[1]
             where = offsets[:, a // STRIPE : (a + n) // STRIPE]
             nc.vector.tensor_tensor(windows[k][:].indirect(where), values, weights, ALU.mult)
 
@@ -192,23 +201,28 @@ def tile_picked_place_lin_gelu_srt_l_kernel(tc, xT, w, b, gate, offs, out):
             activate(0, A, values0_a, a, GROUP)
         product(0, B, 4)
         activate(0, B, values0_b, 0, GROUP)
-        interleave_x(on_vector, 1, 0, 0, CUT_OF_1)
-        place(0, A, values0_a[:])
+        interleave_x(on_vector, 1, 0, 0, GROUP)
+        interleave_x(on_vector, 1, 0, GROUP, CUT_OF_1 - GROUP)
+        quantize_x(1, 0, GROUP)
+        product(1, A, 5, 0, GROUP)
+        gate0, gate1 = spread_gates[:, 0:CHUNK], spread_gates[:, CHUNK:HALF]
+        place(0, A, values0_a[:], gate0)
         in_two(1, CUT_OF_1, CUT_OF_1, CHUNK - CUT_OF_1)
-        quantize_x(1)
-        product(1, A, 5)
+        quantize_x(1, GROUP, GROUP)
+        product(1, A, None, GROUP, GROUP)
         product(1, B, 6)
         activate(0, B, values0_b, GROUP, GROUP, at=0)
-        place(0, B, values0_b)
+        place(0, B, values0_b, gate0)
         in_two(2, 0, 0, GROUP)
         activate(1, A, values1_a)
-        place(1, A, values1_a)
+        place(1, A, values1_a, gate1)
         store(A, 0, HALF)
+        load_gate(3)
         in_two(2, GROUP, GROUP, GROUP)
         quantize_x(2)
         product(2, A, 7)
         activate(1, B, values1_b)
-        place(1, B, values1_b)
+        place(1, B, values1_b, gate1)
         store(B, 0, HALF)
 
         interleave_x(on_vector, 3, 0, CHUNK - VECTOR_OF_3, VECTOR_OF_3)
@@ -219,15 +233,15 @@ def tile_picked_place_lin_gelu_srt_l_kernel(tc, xT, w, b, gate, offs, out):
             product(3, A, a // GROUP, a, GROUP)
         product(3, B, 2)
         activate(2, A, values2_a)
-        place(2, A, values2_a)
+        place(2, A, values2_a, late_gates[:, 0:CHUNK])
         values3_a = keep.tile([P, CHUNK], F32, name="values3_a")
         for a in halves:
             activate(3, A, values3_a, a, GROUP)
-        place(3, A, values3_a[:])
+        place(3, A, values3_a[:], late_gates[:, CHUNK:HALF])
         product(2, B, 1)
         store(A, HALF, T)
         values_b = keep.tile([P, HALF], F32, name="values_b")
         activate(2, B, values_b[:, 0:CHUNK])
         activate(3, B, values_b[:, CHUNK:HALF])
-        place(2, B, values_b[:], HALF)
+        place(2, B, values_b[:], late_gates)
         store(B, HALF, T)

@@ -32,6 +32,7 @@ SCALAR_OF_0 = 160
 CUT_OF_1 = 352
 VECTOR_OF_3 = 96
 LENT = 64
+LATE_CLEARS = 1152
 SCALAR_CLEARS = 1024
 A, B = 0, 1
 
@@ -50,6 +51,13 @@ def tile_picked_place_lin_gelu_srt_l_kernel(tc, xT, w, b, gate, offs, out):
 
         windows = [keep.tile([P, T], F32, name="window%d" % k, align_bytes=64) for k in range(BLOCKS)]
         grouped = [keep.tile([P, CHUNK * PACK], BF16, name="grouped%d" % c, align_bytes=64) for c in range(CHUNKS)]
+        lent_group = windows[B][:, T - GROUP * PACK // 2 : T].bitcast(BF16)
+
+        def rounded(c, a, n):
+            if c == 1 and a < GROUP:
+                return lent_group[:, PACK * a : PACK * (a + n)]
+            return grouped[c][:, PACK * a : PACK * (a + n)]
+
         codes = [keep.tile([P, CHUNK], U32, name="codes%d" % c, align_bytes=64) for c in range(CHUNKS)]
         scales = [keep.tile([P, CHUNK], U8, name="scales%d" % c, align_bytes=64) for c in range(CHUNKS)]
         gate_row = keep.tile([P, GATE_RUN], F32, name="gate_row")
@@ -132,13 +140,13 @@ def tile_picked_place_lin_gelu_srt_l_kernel(tc, xT, w, b, gate, offs, out):
             )
 
         def interleave_x(copy, c, at, a, n):
-            interleave(copy, raw[c, at][:, :, a - at : a - at + n], grouped[c][:, PACK * a : PACK * (a + n)])
+            interleave(copy, raw[c, at][:, :, a - at : a - at + n], rounded(c, a, n))
 
         def quantize(words, scale_bytes, source):
             nc.vector.quantize_mx(out=words.bitcast(FP8X4), scales=scale_bytes, in_=source)
 
         def quantize_x(c, a=0, n=CHUNK):
-            quantize(codes[c][:, a : a + n], scales[c][:, a : a + n], grouped[c][:, PACK * a : PACK * (a + n)])
+            quantize(codes[c][:, a : a + n], scales[c][:, a : a + n], rounded(c, a, n))
 
         sums = {}
 
@@ -178,7 +186,7 @@ def tile_picked_place_lin_gelu_srt_l_kernel(tc, xT, w, b, gate, offs, out):
         nc.vector.memset(windows[A][:, 0:CHUNK], 0.0)
         clear(A, CHUNK, HALF)
         clear(A, HALF, T)
-        clear(B, SCALAR_CLEARS, T)
+        clear(B, SCALAR_CLEARS, T - LATE_CLEARS)
         zeros = windows[A][:, 0:CHUNK].unsqueeze(1).to_broadcast([P, SCALAR_CLEARS // CHUNK, CHUNK])
         cleared = windows[B][:, 0:SCALAR_CLEARS].rearrange("p (n s) -> p n s", s=CHUNK)
         nc.scalar.activation(out=cleared, in_=zeros, func=GELU)
@@ -205,6 +213,7 @@ def tile_picked_place_lin_gelu_srt_l_kernel(tc, xT, w, b, gate, offs, out):
         interleave_x(on_vector, 1, 0, GROUP, CUT_OF_1 - GROUP)
         quantize_x(1, 0, GROUP)
         product(1, A, 5, 0, GROUP)
+        nc.gpsimd.memset(windows[B][:, T - LATE_CLEARS : T], 0.0)
         gate0, gate1 = spread_gates[:, 0:CHUNK], spread_gates[:, CHUNK:HALF]
         place(0, A, values0_a[:], gate0)
         in_two(1, CUT_OF_1, CUT_OF_1, CHUNK - CUT_OF_1)

@@ -28,9 +28,8 @@ RUN = 4
 SCALAR_RUN = 2
 BIAS_PITCH = 8
 GATE_RUN = HALF // P
-SCALAR_OF_0 = 160
-CUT_OF_1 = 352
-VECTOR_OF_3 = 96
+SCALAR_OF_0 = 192
+CUT_OF_1 = 320
 LENT = 64
 LATE_CLEARS = 1152
 SCALAR_CLEARS = 1024
@@ -79,7 +78,7 @@ def tile_picked_place_lin_gelu_srt_l_kernel(tc, xT, w, b, gate, offs, out):
         late_gates, raw[2, 0] = lend("late_gates", LENT, GROUP, lead=CHUNK)
         values1_a = late_gates[:, CHUNK:HALF]
         values1_b, raw[2, GROUP] = lend("values1_b", LENT, GROUP)
-        values2_a, raw[3, 0] = lend("values2_a", GROUP + LENT, CHUNK)
+        values2_a, raw[3, GROUP] = lend("values2_a", LENT, GROUP)
 
         def load_x(c, a, n):
             if (c, a) not in raw:
@@ -96,7 +95,8 @@ def tile_picked_place_lin_gelu_srt_l_kernel(tc, xT, w, b, gate, offs, out):
         load_x(1, CUT_OF_1, CHUNK - CUT_OF_1)
         load_x(2, 0, GROUP)
         load_x(2, GROUP, GROUP)
-        load_x(3, 0, CHUNK)
+        load_x(3, 0, GROUP)
+        load_x(3, GROUP, GROUP)
 
         def load_gate(c):
             nc.sync.dma_start(late_gates[:, (c - 2) * CHUNK : (c - 1) * CHUNK], gate[0:P, c * CHUNK : (c + 1) * CHUNK])
@@ -234,9 +234,8 @@ def tile_picked_place_lin_gelu_srt_l_kernel(tc, xT, w, b, gate, offs, out):
         place(1, B, values1_b, gate1)
         store(B, 0, HALF)
 
-        interleave_x(on_vector, 3, 0, CHUNK - VECTOR_OF_3, VECTOR_OF_3)
         interleave_x(on_scalar, 3, 0, 0, GROUP)
-        in_two(3, 0, GROUP, GROUP - VECTOR_OF_3)
+        in_two(3, GROUP, GROUP, GROUP)
         for a in halves:
             quantize_x(3, a, GROUP)
             product(3, A, a // GROUP, a, GROUP)

@@ -31,7 +31,7 @@ GATE_RUN = HALF // P
 SCALAR_OF_0 = 192
 CUT_OF_1 = 320
 LENT = 64
-LATE_CLEARS = 1152
+LATE_CLEARS = 640
 SCALAR_CLEARS = 1024
 A, B = 0, 1
 
@@ -50,7 +50,9 @@ def tile_picked_place_lin_gelu_srt_l_kernel(tc, xT, w, b, gate, offs, out):
 
         windows = [keep.tile([P, T], F32, name="window%d" % k, align_bytes=64) for k in range(BLOCKS)]
         grouped = [keep.tile([P, CHUNK * PACK], BF16, name="grouped%d" % c, align_bytes=64) for c in range(CHUNKS)]
-        lent_group = windows[B][:, T - GROUP * PACK // 2 : T].bitcast(BF16)
+        last_cleared = T - LATE_CLEARS
+        first_cleared = last_cleared - LATE_CLEARS
+        lent_group = windows[B][:, last_cleared - GROUP * PACK // 2 : last_cleared].bitcast(BF16)
 
         def rounded(c, a, n):
             if c == 1 and a < GROUP:
@@ -186,7 +188,7 @@ def tile_picked_place_lin_gelu_srt_l_kernel(tc, xT, w, b, gate, offs, out):
         nc.vector.memset(windows[A][:, 0:CHUNK], 0.0)
         clear(A, CHUNK, HALF)
         clear(A, HALF, T)
-        clear(B, SCALAR_CLEARS, T - LATE_CLEARS)
+        clear(B, SCALAR_CLEARS, first_cleared)
         zeros = windows[A][:, 0:CHUNK].unsqueeze(1).to_broadcast([P, SCALAR_CLEARS // CHUNK, CHUNK])
         cleared = windows[B][:, 0:SCALAR_CLEARS].rearrange("p (n s) -> p n s", s=CHUNK)
         nc.scalar.activation(out=cleared, in_=zeros, func=GELU)
@@ -213,7 +215,7 @@ def tile_picked_place_lin_gelu_srt_l_kernel(tc, xT, w, b, gate, offs, out):
         interleave_x(on_vector, 1, 0, GROUP, CUT_OF_1 - GROUP)
         quantize_x(1, 0, GROUP)
         product(1, A, 5, 0, GROUP)
-        nc.gpsimd.memset(windows[B][:, T - LATE_CLEARS : T], 0.0)
+        nc.gpsimd.memset(windows[B][:, first_cleared:last_cleared], 0.0)
         gate0, gate1 = spread_gates[:, 0:CHUNK], spread_gates[:, CHUNK:HALF]
         place(0, A, values0_a[:], gate0)
         in_two(1, CUT_OF_1, CUT_OF_1, CHUNK - CUT_OF_1)
@@ -222,6 +224,7 @@ def tile_picked_place_lin_gelu_srt_l_kernel(tc, xT, w, b, gate, offs, out):
         product(1, B, 6)
         activate(0, B, values0_b, GROUP, GROUP, at=0)
         place(0, B, values0_b, gate0)
+        nc.gpsimd.memset(windows[B][:, last_cleared:T], 0.0)
         in_two(2, 0, 0, GROUP)
         activate(1, A, values1_a)
         place(1, A, values1_a, gate1)

@@ -27,11 +27,12 @@ HALF = S // 2
 RUN = 4
 SCALAR_RUN = 2
 BIAS_PITCH = 8
-GATE_RUN = HALF // P
+SPREAD = 3 * CHUNK
+GATE_RUN = SPREAD // P
 SCALAR_OF_0 = 192
 CUT_OF_1 = 320
 LENT = 64
-LATE_CLEARS = 640
+LATE_CLEARS = 1024
 SCALAR_CLEARS = 1024
 A, B = 0, 1
 
@@ -62,7 +63,6 @@ def tile_picked_place_lin_gelu_srt_l_kernel(tc, xT, w, b, gate, offs, out):
         codes = [keep.tile([P, CHUNK], U32, name="codes%d" % c, align_bytes=64) for c in range(CHUNKS)]
         scales = [keep.tile([P, CHUNK], U8, name="scales%d" % c, align_bytes=64) for c in range(CHUNKS)]
         gate_row = keep.tile([P, GATE_RUN], F32, name="gate_row")
-        spread_gates = keep.tile([P, HALF], F32, name="spread_gates")
         w_raw = keep.tile([P, PACK, N], F32, name="w_raw")
         w_grouped = keep.tile([P, N * PACK], BF16, name="w_grouped", align_bytes=64)
         w_codes = keep.tile([P, N], U32, name="w_codes", align_bytes=64)
@@ -77,8 +77,8 @@ def tile_picked_place_lin_gelu_srt_l_kernel(tc, xT, w, b, gate, offs, out):
             return both[:, 0:end], both[:, end - lent :].rearrange("p (t s) -> p t s", t=PACK)
 
         values0_b, raw[1, CUT_OF_1] = lend("values0_b", LENT, CHUNK - CUT_OF_1)
-        late_gates, raw[2, 0] = lend("late_gates", LENT, GROUP, lead=CHUNK)
-        values1_a = late_gates[:, CHUNK:HALF]
+        gates, raw[2, 0] = lend("gates", LENT, GROUP, lead=SPREAD)
+        values1_a = gates[:, SPREAD:S]
         values1_b, raw[2, GROUP] = lend("values1_b", LENT, GROUP)
         values2_a, raw[3, GROUP] = lend("values2_a", LENT, GROUP)
 
@@ -88,7 +88,7 @@ def tile_picked_place_lin_gelu_srt_l_kernel(tc, xT, w, b, gate, offs, out):
             first = c * CHUNK + a
             nc.sync.dma_start(raw[c, a], x_hbm[:, :, first : first + n])
 
-        nc.sync.dma_start(gate_row[:], gate[0:1, 0:HALF].rearrange("o (p i) -> p (o i)", p=P))
+        nc.sync.dma_start(gate_row[:], gate[0:1, 0:SPREAD].rearrange("o (p i) -> p (o i)", p=P))
         nc.sync.dma_start(w_raw[:], w_hbm)
         load_x(0, 0, CHUNK)
         load_x(1, 0, CUT_OF_1)
@@ -99,11 +99,6 @@ def tile_picked_place_lin_gelu_srt_l_kernel(tc, xT, w, b, gate, offs, out):
         load_x(2, GROUP, GROUP)
         load_x(3, 0, GROUP)
         load_x(3, GROUP, GROUP)
-
-        def load_gate(c):
-            nc.sync.dma_start(late_gates[:, (c - 2) * CHUNK : (c - 1) * CHUNK], gate[0:P, c * CHUNK : (c + 1) * CHUNK])
-
-        load_gate(2)
 
         def bank(number, name):
             return psum.tile([P, CHUNK], F32, name=name, tag="bank%d" % number)
@@ -125,14 +120,14 @@ def tile_picked_place_lin_gelu_srt_l_kernel(tc, xT, w, b, gate, offs, out):
                 n = min(HALF, last - a)
                 nc.vector.tensor_copy(out=windows[k][:, a : a + n], in_=windows[A][:, 0:n])
 
-        def spread_gate(u):
+        def spread_gate(u, copy):
             spread = bank(u, "spread%d" % u)
             for r in range(RUN):
                 i = RUN * u + r
                 column = gate_row[:, i : i + 1].to_broadcast([P, P])
                 nc.tensor.transpose(spread[:, r * P : (r + 1) * P], column, identity[:])
-            target = spread_gates[:].rearrange("q (p u r) -> q u p r", u=GATE_RUN // RUN, r=RUN)
-            nc.scalar.copy(out=target[:, u], in_=spread[:].rearrange("q (r p) -> q p r", r=RUN))
+            target = gates[:, 0:SPREAD].rearrange("q (p u r) -> q u p r", u=GATE_RUN // RUN, r=RUN)
+            copy(out=target[:, u], in_=spread[:].rearrange("q (r p) -> q p r", r=RUN))
 
         def interleave(copy, source, target):
             engine, run = copy
@@ -194,7 +189,8 @@ def tile_picked_place_lin_gelu_srt_l_kernel(tc, xT, w, b, gate, offs, out):
         nc.scalar.activation(out=cleared, in_=zeros, func=GELU)
         interleave(on_scalar, w_raw[:], w_grouped[:])
         quantize(w_codes[:], w_scales[:], w_grouped[:])
-        spread_gate(0)
+        spread_gate(0, nc.scalar.copy)
+        spread_gate(1, nc.vector.tensor_copy)
 
         def in_two(c, at, a, n):
             interleave_x(on_scalar, c, at, a, n // 2)
@@ -203,25 +199,25 @@ def tile_picked_place_lin_gelu_srt_l_kernel(tc, xT, w, b, gate, offs, out):
         interleave_x(on_vector, 0, 0, 0, GROUP)
         interleave_x(on_vector, 0, 0, GROUP, GROUP - SCALAR_OF_0)
         interleave_x(on_scalar, 0, 0, CHUNK - SCALAR_OF_0, SCALAR_OF_0)
-        spread_gate(1)
+        spread_gate(2, nc.scalar.copy)
         values0_a = keep.tile([P, CHUNK], F32, name="values0_a")
         for a in halves:
             quantize_x(0, a, GROUP)
-            product(0, A, 2 + a // GROUP, a, GROUP)
+            product(0, A, 3 + a // GROUP, a, GROUP)
             activate(0, A, values0_a, a, GROUP)
-        product(0, B, 4)
+        product(0, B, 5)
         activate(0, B, values0_b, 0, GROUP)
         interleave_x(on_vector, 1, 0, 0, GROUP)
         interleave_x(on_vector, 1, 0, GROUP, CUT_OF_1 - GROUP)
         quantize_x(1, 0, GROUP)
-        product(1, A, 5, 0, GROUP)
+        product(1, A, 6, 0, GROUP)
         nc.gpsimd.memset(windows[B][:, first_cleared:last_cleared], 0.0)
-        gate0, gate1 = spread_gates[:, 0:CHUNK], spread_gates[:, CHUNK:HALF]
+        gate0, gate1 = gates[:, 0:CHUNK], gates[:, CHUNK:HALF]
         place(0, A, values0_a[:], gate0)
         in_two(1, CUT_OF_1, CUT_OF_1, CHUNK - CUT_OF_1)
         quantize_x(1, GROUP, GROUP)
         product(1, A, None, GROUP, GROUP)
-        product(1, B, 6)
+        product(1, B, 7)
         activate(0, B, values0_b, GROUP, GROUP, at=0)
         place(0, B, values0_b, gate0)
         nc.gpsimd.memset(windows[B][:, last_cleared:T], 0.0)
@@ -229,10 +225,10 @@ def tile_picked_place_lin_gelu_srt_l_kernel(tc, xT, w, b, gate, offs, out):
         activate(1, A, values1_a)
         place(1, A, values1_a, gate1)
         store(A, 0, HALF)
-        load_gate(3)
+        nc.sync.dma_start(gates[:, SPREAD:S], gate[0:P, SPREAD:S])
         in_two(2, GROUP, GROUP, GROUP)
         quantize_x(2)
-        product(2, A, 7)
+        product(2, A, 2)
         activate(1, B, values1_b)
         place(1, B, values1_b, gate1)
         store(B, 0, HALF)
@@ -242,17 +238,17 @@ def tile_picked_place_lin_gelu_srt_l_kernel(tc, xT, w, b, gate, offs, out):
         for a in halves:
             quantize_x(3, a, GROUP)
             product(3, A, a // GROUP, a, GROUP)
-        product(3, B, 2)
+        product(3, B, 3)
         activate(2, A, values2_a)
-        place(2, A, values2_a, late_gates[:, 0:CHUNK])
+        place(2, A, values2_a, gates[:, HALF:SPREAD])
         values3_a = keep.tile([P, CHUNK], F32, name="values3_a")
         for a in halves:
             activate(3, A, values3_a, a, GROUP)
-        place(3, A, values3_a[:], late_gates[:, CHUNK:HALF])
+        place(3, A, values3_a[:], gates[:, SPREAD:S])
         product(2, B, 1)
         store(A, HALF, T)
         values_b = keep.tile([P, HALF], F32, name="values_b")
         activate(2, B, values_b[:, 0:CHUNK])
         activate(3, B, values_b[:, CHUNK:HALF])
-        place(2, B, values_b[:], late_gates)
+        place(2, B, values_b[:], gates[:, HALF:S])
         store(B, HALF, T)

@@ -32,6 +32,7 @@ GATE_RUN = SPREAD // P
 SCALAR_OF_0 = 192
 CUT_OF_1 = 320
 LENT = 64
+VECTOR_OF_2 = 64
 LATE_CLEARS = 1024
 SCALAR_CLEARS = 1024
 A, B = 0, 1
@@ -71,16 +72,21 @@ def tile_picked_place_lin_gelu_srt_l_kernel(tc, xT, w, b, gate, offs, out):
 
         raw = {}
 
-        def lend(name, lent, n, lead=0):
-            end = lead + CHUNK
-            both = keep.tile([P, end - lent + PACK * n], F32, name=name, align_bytes=64)
-            return both[:, 0:end], both[:, end - lent :].rearrange("p (t s) -> p t s", t=PACK)
+        def chained(name, *widths):
+            whole = keep.tile([P, sum(widths) - LENT * (len(widths) - 1)], F32, name=name, align_bytes=64)
+            starts = [sum(widths[:i]) - LENT * i for i in range(len(widths))]
+            return [whole[:, a : a + n] for a, n in zip(starts, widths)]
 
-        values0_b, raw[1, CUT_OF_1] = lend("values0_b", LENT, CHUNK - CUT_OF_1)
-        gates, raw[2, 0] = lend("gates", LENT, GROUP, lead=SPREAD)
-        values1_a = gates[:, SPREAD:S]
-        values1_b, raw[2, GROUP] = lend("values1_b", LENT, GROUP)
-        values2_a, raw[3, GROUP] = lend("values2_a", LENT, GROUP)
+        def planes(run):
+            return run.rearrange("p (t s) -> p t s", t=PACK)
+
+        values0_b, run1, values1_a, run2 = chained("early", CHUNK, PACK * (CHUNK - CUT_OF_1), CHUNK, PACK * GROUP)
+        raw[1, CUT_OF_1], raw[2, 0] = planes(run1), planes(run2)
+        gates, run2 = chained("gates", S, PACK * GROUP)
+        values1_b = gates[:, SPREAD:S]
+        raw[2, GROUP] = planes(run2)
+        values2_a, run3, values_b = chained("late", CHUNK, PACK * GROUP, HALF)
+        raw[3, GROUP] = planes(run3)
 
         def load_x(c, a, n):
             if (c, a) not in raw:
@@ -214,41 +220,44 @@ def tile_picked_place_lin_gelu_srt_l_kernel(tc, xT, w, b, gate, offs, out):
         nc.gpsimd.memset(windows[B][:, first_cleared:last_cleared], 0.0)
         gate0, gate1 = gates[:, 0:CHUNK], gates[:, CHUNK:HALF]
         place(0, A, values0_a[:], gate0)
-        in_two(1, CUT_OF_1, CUT_OF_1, CHUNK - CUT_OF_1)
+        rest = (CHUNK - CUT_OF_1) // 2
+        interleave_x(on_scalar, 1, CUT_OF_1, CUT_OF_1 + rest, rest)
+        interleave_x(on_scalar, 1, CUT_OF_1, CUT_OF_1, rest)
+        activate(1, A, values1_a, 0, GROUP)
         quantize_x(1, GROUP, GROUP)
-        product(1, A, None, GROUP, GROUP)
-        product(1, B, 7)
+        product(1, A, 7, GROUP, GROUP)
+        product(1, B, 0)
         activate(0, B, values0_b, GROUP, GROUP, at=0)
         place(0, B, values0_b, gate0)
         nc.gpsimd.memset(windows[B][:, last_cleared:T], 0.0)
-        in_two(2, 0, 0, GROUP)
-        activate(1, A, values1_a)
+        in_two(2, 0, 0, GROUP - VECTOR_OF_2)
+        interleave_x(on_vector, 2, 0, GROUP - VECTOR_OF_2, VECTOR_OF_2)
+        activate(1, A, values1_a, GROUP, GROUP)
         place(1, A, values1_a, gate1)
         store(A, 0, HALF)
-        nc.sync.dma_start(gates[:, SPREAD:S], gate[0:P, SPREAD:S])
         in_two(2, GROUP, GROUP, GROUP)
         quantize_x(2)
-        product(2, A, 2)
+        product(2, A, 1)
+        product(2, B, 2)
         activate(1, B, values1_b)
         place(1, B, values1_b, gate1)
+        nc.sync.dma_start(gates[:, SPREAD:S], gate[0:P, SPREAD:S])
         store(B, 0, HALF)
 
         interleave_x(on_scalar, 3, 0, 0, GROUP)
         in_two(3, GROUP, GROUP, GROUP)
         for a in halves:
             quantize_x(3, a, GROUP)
-            product(3, A, a // GROUP, a, GROUP)
-        product(3, B, 3)
+            product(3, A, 3 + a // GROUP, a, GROUP)
+        product(3, B, 5)
         activate(2, A, values2_a)
         place(2, A, values2_a, gates[:, HALF:SPREAD])
+        activate(2, B, values_b[:, 0:CHUNK])
         values3_a = keep.tile([P, CHUNK], F32, name="values3_a")
         for a in halves:
             activate(3, A, values3_a, a, GROUP)
         place(3, A, values3_a[:], gates[:, SPREAD:S])
-        product(2, B, 1)
         store(A, HALF, T)
-        values_b = keep.tile([P, HALF], F32, name="values_b")
-        activate(2, B, values_b[:, 0:CHUNK])
         activate(3, B, values_b[:, CHUNK:HALF])
-        place(2, B, values_b[:], gates[:, HALF:S])
+        place(2, B, values_b, gates[:, HALF:S])
         store(B, HALF, T)

@@ -27,12 +27,12 @@ HALF = S // 2
 RUN = 4
 SCALAR_RUN = 2
 BIAS_PITCH = 8
-SPREAD = 3 * CHUNK
-GATE_RUN = SPREAD // P
+GATE_RUN = S // P
 SCALAR_OF_0 = 192
 CUT_OF_1 = 320
 LENT = 64
 VECTOR_OF_2 = 64
+LATE_GATES = 2 * RUN
 LATE_CLEARS = 1024
 SCALAR_CLEARS = 1024
 A, B = 0, 1
@@ -72,20 +72,21 @@ def tile_picked_place_lin_gelu_srt_l_kernel(tc, xT, w, b, gate, offs, out):
 
         raw = {}
 
-        def chained(name, *widths):
-            whole = keep.tile([P, sum(widths) - LENT * (len(widths) - 1)], F32, name=name, align_bytes=64)
-            starts = [sum(widths[:i]) - LENT * i for i in range(len(widths))]
+        def chained(name, lent, *widths):
+            whole = keep.tile([P, sum(widths) - lent * (len(widths) - 1)], F32, name=name, align_bytes=64)
+            starts = [sum(widths[:i]) - lent * i for i in range(len(widths))]
             return [whole[:, a : a + n] for a, n in zip(starts, widths)]
 
         def planes(run):
             return run.rearrange("p (t s) -> p t s", t=PACK)
 
-        values0_b, run1, values1_a, run2 = chained("early", CHUNK, PACK * (CHUNK - CUT_OF_1), CHUNK, PACK * GROUP)
+        values0_b, run1, values1_a, run2 = chained("early", LENT, CHUNK, PACK * (CHUNK - CUT_OF_1), CHUNK, PACK * GROUP)
         raw[1, CUT_OF_1], raw[2, 0] = planes(run1), planes(run2)
-        gates, run2 = chained("gates", S, PACK * GROUP)
-        values1_b = gates[:, SPREAD:S]
+        gates, run0 = chained("gates", LATE_GATES, S, PACK * CHUNK)
+        raw[0, 0] = planes(run0)
+        values1_b, run2 = chained("middle", LENT, CHUNK, PACK * GROUP)
         raw[2, GROUP] = planes(run2)
-        values2_a, run3, values_b = chained("late", CHUNK, PACK * GROUP, HALF)
+        values2_a, run3, values_b = chained("late", LENT, CHUNK, PACK * GROUP, HALF)
         raw[3, GROUP] = planes(run3)
 
         def load_x(c, a, n):
@@ -94,7 +95,7 @@ def tile_picked_place_lin_gelu_srt_l_kernel(tc, xT, w, b, gate, offs, out):
             first = c * CHUNK + a
             nc.sync.dma_start(raw[c, a], x_hbm[:, :, first : first + n])
 
-        nc.sync.dma_start(gate_row[:], gate[0:1, 0:SPREAD].rearrange("o (p i) -> p (o i)", p=P))
+        nc.sync.dma_start(gate_row[:], gate[0:1, :].rearrange("o (p i) -> p (o i)", p=P))
         nc.sync.dma_start(w_raw[:], w_hbm)
         load_x(0, 0, CHUNK)
         load_x(1, 0, CUT_OF_1)
@@ -132,7 +133,7 @@ def tile_picked_place_lin_gelu_srt_l_kernel(tc, xT, w, b, gate, offs, out):
                 i = RUN * u + r
                 column = gate_row[:, i : i + 1].to_broadcast([P, P])
                 nc.tensor.transpose(spread[:, r * P : (r + 1) * P], column, identity[:])
-            target = gates[:, 0:SPREAD].rearrange("q (p u r) -> q u p r", u=GATE_RUN // RUN, r=RUN)
+            target = gates.rearrange("q (p u r) -> q u p r", u=GATE_RUN // RUN, r=RUN)
             copy(out=target[:, u], in_=spread[:].rearrange("q (r p) -> q p r", r=RUN))
 
         def interleave(copy, source, target):
@@ -202,21 +203,22 @@ def tile_picked_place_lin_gelu_srt_l_kernel(tc, xT, w, b, gate, offs, out):
             interleave_x(on_scalar, c, at, a, n // 2)
             interleave_x(on_scalar, c, at, a + n // 2, n // 2)
 
-        interleave_x(on_vector, 0, 0, 0, GROUP)
-        interleave_x(on_vector, 0, 0, GROUP, GROUP - SCALAR_OF_0)
-        interleave_x(on_scalar, 0, 0, CHUNK - SCALAR_OF_0, SCALAR_OF_0)
+        interleave_x(on_vector, 0, 0, GROUP, GROUP)
+        interleave_x(on_vector, 0, 0, SCALAR_OF_0, GROUP - SCALAR_OF_0)
+        in_two(0, 0, 0, SCALAR_OF_0)
         spread_gate(2, nc.scalar.copy)
+        spread_gate(3, nc.scalar.copy)
         values0_a = keep.tile([P, CHUNK], F32, name="values0_a")
-        for a in halves:
+        for a in reversed(halves):
             quantize_x(0, a, GROUP)
-            product(0, A, 3 + a // GROUP, a, GROUP)
+            product(0, A, 4 + a // GROUP, a, GROUP)
             activate(0, A, values0_a, a, GROUP)
-        product(0, B, 5)
+        product(0, B, 6)
         activate(0, B, values0_b, 0, GROUP)
         interleave_x(on_vector, 1, 0, 0, GROUP)
         interleave_x(on_vector, 1, 0, GROUP, CUT_OF_1 - GROUP)
         quantize_x(1, 0, GROUP)
-        product(1, A, 6, 0, GROUP)
+        product(1, A, 7, 0, GROUP)
         nc.gpsimd.memset(windows[B][:, first_cleared:last_cleared], 0.0)
         gate0, gate1 = gates[:, 0:CHUNK], gates[:, CHUNK:HALF]
         place(0, A, values0_a[:], gate0)
@@ -225,8 +227,8 @@ def tile_picked_place_lin_gelu_srt_l_kernel(tc, xT, w, b, gate, offs, out):
         interleave_x(on_scalar, 1, CUT_OF_1, CUT_OF_1, rest)
         activate(1, A, values1_a, 0, GROUP)
         quantize_x(1, GROUP, GROUP)
-        product(1, A, 7, GROUP, GROUP)
-        product(1, B, 0)
+        product(1, A, 0, GROUP, GROUP)
+        product(1, B, 1)
         activate(0, B, values0_b, GROUP, GROUP, at=0)
         place(0, B, values0_b, gate0)
         nc.gpsimd.memset(windows[B][:, last_cleared:T], 0.0)
@@ -237,26 +239,25 @@ def tile_picked_place_lin_gelu_srt_l_kernel(tc, xT, w, b, gate, offs, out):
         store(A, 0, HALF)
         in_two(2, GROUP, GROUP, GROUP)
         quantize_x(2)
-        product(2, A, 1)
-        product(2, B, 2)
+        product(2, A, 2)
+        product(2, B, 3)
         activate(1, B, values1_b)
         place(1, B, values1_b, gate1)
-        nc.sync.dma_start(gates[:, SPREAD:S], gate[0:P, SPREAD:S])
         store(B, 0, HALF)
 
         interleave_x(on_scalar, 3, 0, 0, GROUP)
         in_two(3, GROUP, GROUP, GROUP)
         for a in halves:
             quantize_x(3, a, GROUP)
-            product(3, A, 3 + a // GROUP, a, GROUP)
-        product(3, B, 5)
+            product(3, A, 4 + a // GROUP, a, GROUP)
+        product(3, B, 6)
         activate(2, A, values2_a)
-        place(2, A, values2_a, gates[:, HALF:SPREAD])
+        place(2, A, values2_a, gates[:, HALF : HALF + CHUNK])
         activate(2, B, values_b[:, 0:CHUNK])
         values3_a = keep.tile([P, CHUNK], F32, name="values3_a")
         for a in halves:
             activate(3, A, values3_a, a, GROUP)
-        place(3, A, values3_a[:], gates[:, SPREAD:S])
+        place(3, A, values3_a[:], gates[:, HALF + CHUNK : S])
         store(A, HALF, T)
         activate(3, B, values_b[:, CHUNK:HALF])
         place(2, B, values_b, gates[:, HALF:S])

@@ -29,9 +29,8 @@ SCALAR_RUN = 2
 BIAS_PITCH = 8
 GATE_RUN = S // P
 SCALAR_OF_0 = 192
-CUT_OF_1 = 320
+CUT_OF_1 = 384
 LENT = 64
-VECTOR_OF_2 = 64
 LATE_GATES = 2 * RUN
 LATE_CLEARS = 1024
 SCALAR_CLEARS = 1024
@@ -54,10 +53,10 @@ def tile_picked_place_lin_gelu_srt_l_kernel(tc, xT, w, b, gate, offs, out):
         grouped = [keep.tile([P, CHUNK * PACK], BF16, name="grouped%d" % c, align_bytes=64) for c in range(CHUNKS)]
         last_cleared = T - LATE_CLEARS
         first_cleared = last_cleared - LATE_CLEARS
-        lent_group = windows[B][:, last_cleared - GROUP * PACK // 2 : last_cleared].bitcast(BF16)
+        lent_group = windows[B][:, last_cleared - CUT_OF_1 * PACK // 2 : last_cleared].bitcast(BF16)
 
         def rounded(c, a, n):
-            if c == 1 and a < GROUP:
+            if c == 1 and a < CUT_OF_1:
                 return lent_group[:, PACK * a : PACK * (a + n)]
             return grouped[c][:, PACK * a : PACK * (a + n)]
 
@@ -214,27 +213,25 @@ def tile_picked_place_lin_gelu_srt_l_kernel(tc, xT, w, b, gate, offs, out):
             product(0, A, 4 + a // GROUP, a, GROUP)
             activate(0, A, values0_a, a, GROUP)
         product(0, B, 6)
-        activate(0, B, values0_b, 0, GROUP)
         interleave_x(on_vector, 1, 0, 0, GROUP)
         interleave_x(on_vector, 1, 0, GROUP, CUT_OF_1 - GROUP)
         quantize_x(1, 0, GROUP)
+        quantize_x(1, GROUP, CUT_OF_1 - GROUP)
         product(1, A, 7, 0, GROUP)
+        product(1, A, None, GROUP, CUT_OF_1 - GROUP)
         nc.gpsimd.memset(windows[B][:, first_cleared:last_cleared], 0.0)
         gate0, gate1 = gates[:, 0:CHUNK], gates[:, CHUNK:HALF]
         place(0, A, values0_a[:], gate0)
-        rest = (CHUNK - CUT_OF_1) // 2
-        interleave_x(on_scalar, 1, CUT_OF_1, CUT_OF_1 + rest, rest)
-        interleave_x(on_scalar, 1, CUT_OF_1, CUT_OF_1, rest)
-        activate(1, A, values1_a, 0, GROUP)
-        quantize_x(1, GROUP, GROUP)
-        product(1, A, 0, GROUP, GROUP)
+        in_two(1, CUT_OF_1, CUT_OF_1, CHUNK - CUT_OF_1)
+        activate(0, B, values0_b)
+        activate(1, A, values1_a, 0, CUT_OF_1)
+        quantize_x(1, CUT_OF_1, CHUNK - CUT_OF_1)
+        product(1, A, 0, CUT_OF_1, CHUNK - CUT_OF_1)
         product(1, B, 1)
-        activate(0, B, values0_b, GROUP, GROUP, at=0)
         place(0, B, values0_b, gate0)
         nc.gpsimd.memset(windows[B][:, last_cleared:T], 0.0)
-        in_two(2, 0, 0, GROUP - VECTOR_OF_2)
-        interleave_x(on_vector, 2, 0, GROUP - VECTOR_OF_2, VECTOR_OF_2)
-        activate(1, A, values1_a, GROUP, GROUP)
+        in_two(2, 0, 0, GROUP)
+        activate(1, A, values1_a, CUT_OF_1, CHUNK - CUT_OF_1)
         place(1, A, values1_a, gate1)
         store(A, 0, HALF)
         in_two(2, GROUP, GROUP, GROUP)

@@ -32,7 +32,8 @@ SCALAR_OF_0 = 192
 CUT_OF_1 = 384
 LENT = 64
 LATE_GATES = 2 * RUN
-LATE_CLEARS = 1024
+LATE_CLEARS = 1152
+LATE_CLEARS_A = 896
 SCALAR_CLEARS = 1024
 A, B = 0, 1
 
@@ -122,9 +123,7 @@ def tile_picked_place_lin_gelu_srt_l_kernel(tc, xT, w, b, gate, offs, out):
         nc.vector.tensor_scalar(identity[:], counts[:], quad_start[:, 0:1], lanes[:, 0:1], ALU.subtract, ALU.is_equal)
 
         def clear(k, first, last):
-            for a in range(first, last, HALF):
-                n = min(HALF, last - a)
-                nc.vector.tensor_copy(out=windows[k][:, a : a + n], in_=windows[A][:, 0:n])
+            nc.vector.tensor_copy(out=windows[k][:, first:last], in_=windows[A][:, 0 : last - first])
 
         def spread_gate(u, copy):
             spread = bank(u, "spread%d" % u)
@@ -188,8 +187,9 @@ def tile_picked_place_lin_gelu_srt_l_kernel(tc, xT, w, b, gate, offs, out):
 
         nc.vector.memset(windows[A][:, 0:CHUNK], 0.0)
         clear(A, CHUNK, HALF)
-        clear(A, HALF, T)
+        clear(A, HALF, S)
         clear(B, SCALAR_CLEARS, first_cleared)
+        clear(A, S, T - LATE_CLEARS_A)
         zeros = windows[A][:, 0:CHUNK].unsqueeze(1).to_broadcast([P, SCALAR_CLEARS // CHUNK, CHUNK])
         cleared = windows[B][:, 0:SCALAR_CLEARS].rearrange("p (n s) -> p n s", s=CHUNK)
         nc.scalar.activation(out=cleared, in_=zeros, func=GELU)
@@ -222,6 +222,7 @@ def tile_picked_place_lin_gelu_srt_l_kernel(tc, xT, w, b, gate, offs, out):
         nc.gpsimd.memset(windows[B][:, first_cleared:last_cleared], 0.0)
         gate0, gate1 = gates[:, 0:CHUNK], gates[:, CHUNK:HALF]
         place(0, A, values0_a[:], gate0)
+        nc.gpsimd.memset(windows[A][:, T - LATE_CLEARS_A : T], 0.0)
         in_two(1, CUT_OF_1, CUT_OF_1, CHUNK - CUT_OF_1)
         activate(0, B, values0_b)
         activate(1, A, values1_a, 0, CUT_OF_1)

@@ -32,8 +32,9 @@ SCALAR_OF_0 = 192
 CUT_OF_1 = 384
 LENT = 64
 LATE_GATES = 2 * RUN
-LATE_CLEARS = 1152
-LATE_CLEARS_A = 896
+FIRST_LATE = 896
+LAST_LATE = 1152
+LATE_CLEARS_A = 768
 SCALAR_CLEARS = 1024
 A, B = 0, 1
 
@@ -52,12 +53,12 @@ def tile_picked_place_lin_gelu_srt_l_kernel(tc, xT, w, b, gate, offs, out):
 
         windows = [keep.tile([P, T], F32, name="window%d" % k, align_bytes=64) for k in range(BLOCKS)]
         grouped = [keep.tile([P, CHUNK * PACK], BF16, name="grouped%d" % c, align_bytes=64) for c in range(CHUNKS)]
-        last_cleared = T - LATE_CLEARS
-        first_cleared = last_cleared - LATE_CLEARS
-        lent_group = windows[B][:, last_cleared - CUT_OF_1 * PACK // 2 : last_cleared].bitcast(BF16)
+        last_cleared = T - LAST_LATE
+        first_cleared = last_cleared - FIRST_LATE
+        lent_group = windows[B][:, last_cleared - GROUP * PACK // 2 : last_cleared].bitcast(BF16)
 
         def rounded(c, a, n):
-            if c == 1 and a < CUT_OF_1:
+            if c == 1 and a < GROUP:
                 return lent_group[:, PACK * a : PACK * (a + n)]
             return grouped[c][:, PACK * a : PACK * (a + n)]
 
@@ -187,8 +188,9 @@ def tile_picked_place_lin_gelu_srt_l_kernel(tc, xT, w, b, gate, offs, out):
 
         nc.vector.memset(windows[A][:, 0:CHUNK], 0.0)
         clear(A, CHUNK, HALF)
+        clear(B, SCALAR_CLEARS, SCALAR_CLEARS + CHUNK)
+        clear(B, SCALAR_CLEARS + CHUNK, first_cleared)
         clear(A, HALF, S)
-        clear(B, SCALAR_CLEARS, first_cleared)
         clear(A, S, T - LATE_CLEARS_A)
         zeros = windows[A][:, 0:CHUNK].unsqueeze(1).to_broadcast([P, SCALAR_CLEARS // CHUNK, CHUNK])
         cleared = windows[B][:, 0:SCALAR_CLEARS].rearrange("p (n s) -> p n s", s=CHUNK)

@@ -26,7 +26,6 @@ BLOCKS = N // P
 HALF = S // 2
 RUN = 4
 SCALAR_RUN = 2
-BIAS_PITCH = 8
 GATE_RUN = S // P
 SCALAR_OF_0 = 192
 CUT_OF_1 = 384
@@ -50,6 +49,7 @@ def tile_picked_place_lin_gelu_srt_l_kernel(tc, xT, w, b, gate, offs, out):
 
         x_hbm = xT.rearrange("(p t) s -> p t s", t=PACK)
         w_hbm = w.rearrange("(p t) m -> p t m", t=PACK)
+        out_rows = out.rearrange("(p k) s -> k p s", k=BLOCKS)
 
         windows = [keep.tile([P, T], F32, name="window%d" % k, align_bytes=64) for k in range(BLOCKS)]
         grouped = [keep.tile([P, CHUNK * PACK], BF16, name="grouped%d" % c, align_bytes=64) for c in range(CHUNKS)]
@@ -69,7 +69,7 @@ def tile_picked_place_lin_gelu_srt_l_kernel(tc, xT, w, b, gate, offs, out):
         w_grouped = keep.tile([P, N * PACK], BF16, name="w_grouped", align_bytes=64)
         w_codes = keep.tile([P, N], U32, name="w_codes", align_bytes=64)
         w_scales = keep.tile([P, N], U8, name="w_scales", align_bytes=64)
-        bias = keep.tile([P, BLOCKS, BIAS_PITCH], F32, name="bias")
+        bias = keep.tile([P, BLOCKS], F32, name="bias")
 
         raw = {}
 
@@ -100,7 +100,7 @@ def tile_picked_place_lin_gelu_srt_l_kernel(tc, xT, w, b, gate, offs, out):
         nc.sync.dma_start(w_raw[:], w_hbm)
         load_x(0, 0, CHUNK)
         load_x(1, 0, CUT_OF_1)
-        nc.sync.dma_start(bias[:, :, 0:1], b.rearrange("(k p) o -> p k o", p=P))
+        nc.sync.dma_start(bias[:], b.rearrange("(p k) o -> p (k o)", k=BLOCKS))
         nc.sync.dma_start(offsets[:], offs)
         load_x(1, CUT_OF_1, CHUNK - CUT_OF_1)
         load_x(2, 0, GROUP)
@@ -173,7 +173,7 @@ def tile_picked_place_lin_gelu_srt_l_kernel(tc, xT, w, b, gate, offs, out):
         def activate(c, k, values, a=0, n=CHUNK, at=None):
             at = a if at is None else at
             source = sums[c, k, at][:, a - at : a - at + n]
-            nc.scalar.activation(out=values[:, a : a + n], in_=source, func=GELU, bias=bias[:, k, 0:1])
+            nc.scalar.activation(out=values[:, a : a + n], in_=source, func=GELU, bias=bias[:, k : k + 1])
 
         def place(c, k, values, weights):
             a, n = c * CHUNK, values.shape[1]
@@ -181,7 +181,7 @@ def tile_picked_place_lin_gelu_srt_l_kernel(tc, xT, w, b, gate, offs, out):
             nc.vector.tensor_tensor(windows[k][:].indirect(where), values, weights, ALU.mult)
 
         def store(k, c0, c1):
-            nc.sync.dma_start(out[k * P : (k + 1) * P, c0:c1], windows[k][:, c0:c1])
+            nc.sync.dma_start(out_rows[k, :, c0:c1], windows[k][:, c0:c1])
 
         on_vector, on_scalar = (nc.vector.tensor_copy, RUN), (nc.scalar.copy, SCALAR_RUN)
         halves = (0, GROUP)
@@ -195,7 +195,10 @@ def tile_picked_place_lin_gelu_srt_l_kernel(tc, xT, w, b, gate, offs, out):
         zeros = windows[A][:, 0:CHUNK].unsqueeze(1).to_broadcast([P, SCALAR_CLEARS // CHUNK, CHUNK])
         cleared = windows[B][:, 0:SCALAR_CLEARS].rearrange("p (n s) -> p n s", s=CHUNK)
         nc.scalar.activation(out=cleared, in_=zeros, func=GELU)
-        interleave(on_scalar, w_raw[:], w_grouped[:])
+        nc.scalar.copy(
+            out=w_grouped[:].rearrange("p (k c i t) -> p c t i k", k=BLOCKS, i=SCALAR_RUN, t=PACK),
+            in_=w_raw[:].rearrange("p t (c i k) -> p c t i k", i=SCALAR_RUN, k=BLOCKS),
+        )
         quantize(w_codes[:], w_scales[:], w_grouped[:])
         spread_gate(0, nc.scalar.copy)
         spread_gate(1, nc.vector.tensor_copy)

from contextlib import ExitStack

import concourse.mybir as mybir

K, T, S, N = 512, 4096, 2048, 256
FLOPS = 2 * K * S * N
BYTES = 4 * (K * S + K * N + N + S + N * T) + 2 * S

F32 = mybir.dt.float32
BF16 = mybir.dt.bfloat16
U32 = mybir.dt.uint32
U16 = mybir.dt.uint16
U8 = mybir.dt.uint8
FP8X4 = mybir.dt.float8_e4m3fn_x4
GELU = mybir.ActivationFunctionType.Gelu_apprx_tanh
ALU = mybir.AluOpType

P = 128
QUAD = 32
PACK = 4
STRIPE = 16
CHUNK = 512
CHUNKS = S // CHUNK
GROUP = CHUNK // 2
BLOCKS = N // P
HALF = S // 2
RUN = 4
SCALAR_RUN = 2
GATE_RUN = S // P
SCALAR_OF_0 = 192
CUT_OF_1 = 384
LENT = 64
LATE_GATES = 2 * RUN
FIRST_LATE = 896
LAST_LATE = 1152
LATE_CLEARS_A = 768
SCALAR_CLEARS = 1024
A, B = 0, 1


def tile_picked_place_lin_gelu_srt_l_kernel(tc, xT, w, b, gate, offs, out):
    nc = tc.nc
    with ExitStack() as ctx:
        lists = ctx.enter_context(tc.tile_pool(name="lists", bufs=1))
        keep = ctx.enter_context(tc.tile_pool(name="keep", bufs=1))
        psum = ctx.enter_context(tc.psum_pool(name="psum", bufs=1))

        offsets = lists.tile([P, S // STRIPE], U16, name="offsets")

        x_hbm = xT.rearrange("(p t) s -> p t s", t=PACK)
        w_hbm = w.rearrange("(p t) m -> p t m", t=PACK)
        out_rows = out.rearrange("(p k) s -> k p s", k=BLOCKS)

        windows = [keep.tile([P, T], F32, name="window%d" % k, align_bytes=64) for k in range(BLOCKS)]
        grouped = [keep.tile([P, CHUNK * PACK], BF16, name="grouped%d" % c, align_bytes=64) for c in range(CHUNKS)]
        last_cleared = T - LAST_LATE
        first_cleared = last_cleared - FIRST_LATE
        lent_group = windows[B][:, last_cleared - GROUP * PACK // 2 : last_cleared].bitcast(BF16)

        def rounded(c, a, n):
            if c == 1 and a < GROUP:
                return lent_group[:, PACK * a : PACK * (a + n)]
            return grouped[c][:, PACK * a : PACK * (a + n)]

        codes = [keep.tile([P, CHUNK], U32, name="codes%d" % c, align_bytes=64) for c in range(CHUNKS)]
        scales = [keep.tile([P, CHUNK], U8, name="scales%d" % c, align_bytes=64) for c in range(CHUNKS)]
        gate_row = keep.tile([P, GATE_RUN], F32, name="gate_row")
        w_raw = keep.tile([P, PACK, N], F32, name="w_raw")
        w_grouped = keep.tile([P, N * PACK], BF16, name="w_grouped", align_bytes=64)
        w_codes = keep.tile([P, N], U32, name="w_codes", align_bytes=64)
        w_scales = keep.tile([P, N], U8, name="w_scales", align_bytes=64)
        bias = keep.tile([P, BLOCKS], F32, name="bias")

        raw = {}

        def chained(name, lent, *widths):
            whole = keep.tile([P, sum(widths) - lent * (len(widths) - 1)], F32, name=name, align_bytes=64)
            starts = [sum(widths[:i]) - lent * i for i in range(len(widths))]
            return [whole[:, a : a + n] for a, n in zip(starts, widths)]

        def planes(run):
            return run.rearrange("p (t s) -> p t s", t=PACK)

        values0_b, run1, values1_a, run2 = chained("early", LENT, CHUNK, PACK * (CHUNK - CUT_OF_1), CHUNK, PACK * GROUP)
        raw[1, CUT_OF_1], raw[2, 0] = planes(run1), planes(run2)
        gates, run0 = chained("gates", LATE_GATES, S, PACK * CHUNK)
        raw[0, 0] = planes(run0)
        values1_b, run2 = chained("middle", LENT, CHUNK, PACK * GROUP)
        raw[2, GROUP] = planes(run2)
        values2_a, run3, values_b = chained("late", LENT, CHUNK, PACK * GROUP, HALF)
        raw[3, GROUP] = planes(run3)

        def load_x(c, a, n):
            if (c, a) not in raw:
                raw[c, a] = keep.tile([P, PACK, n], F32, name="raw%d_%d" % (c, a), align_bytes=64)[:]
            first = c * CHUNK + a
            nc.sync.dma_start(raw[c, a], x_hbm[:, :, first : first + n])

        nc.sync.dma_start(gate_row[:], gate[0:1, :].rearrange("o (p i) -> p (o i)", p=P))
        nc.sync.dma_start(w_raw[:], w_hbm)
        load_x(0, 0, CHUNK)
        load_x(1, 0, CUT_OF_1)
        nc.sync.dma_start(bias[:], b.rearrange("(p k) o -> p (k o)", k=BLOCKS))
        nc.sync.dma_start(offsets[:], offs)
        load_x(1, CUT_OF_1, CHUNK - CUT_OF_1)
        load_x(2, 0, GROUP)
        load_x(2, GROUP, GROUP)
        load_x(3, 0, GROUP)
        load_x(3, GROUP, GROUP)

        def bank(number, name):
            return psum.tile([P, CHUNK], F32, name=name, tag="bank%d" % number)

        ones = keep.tile([P, P], F32, name="ones")
        quad_start = keep.tile([P, 1], F32, name="quad_start")
        counts = keep.tile([P, P], F32, name="counts", align_bytes=64)
        lanes = keep.tile([P, QUAD], F32, name="lanes", align_bytes=64)
        identity = keep.tile([P, P], F32, name="identity")
        nc.gpsimd.memset(ones[:], 1.0)
        for q in range(0, P, QUAD):
            nc.gpsimd.memset(quad_start[q : q + QUAD, :], float(q))
        nc.vector.tensor_tensor_scan(counts[:], ones[:], ones[:], 0.0, ALU.mult, ALU.add)
        nc.vector.transpose(lanes[:], counts[:, 0:QUAD])
        nc.vector.tensor_scalar(identity[:], counts[:], quad_start[:, 0:1], lanes[:, 0:1], ALU.subtract, ALU.is_equal)

        def clear(k, first, last):
            nc.vector.tensor_copy(out=windows[k][:, first:last], in_=windows[A][:, 0 : last - first])

        def spread_gate(u, copy):
            spread = bank(u, "spread%d" % u)
            for r in range(RUN):
                i = RUN * u + r
                column = gate_row[:, i : i + 1].to_broadcast([P, P])
                nc.tensor.transpose(spread[:, r * P : (r + 1) * P], column, identity[:])
            target = gates.rearrange("q (p u r) -> q u p r", u=GATE_RUN // RUN, r=RUN)
            copy(out=target[:, u], in_=spread[:].rearrange("q (r p) -> q p r", r=RUN))

        def interleave(copy, source, target):
            engine, run = copy
            engine(
                out=target.rearrange("p (c i t) -> p c t i", i=run, t=PACK),
                in_=source.rearrange("p t (c i) -> p c t i", i=run),
            )

        def interleave_x(copy, c, at, a, n):
            interleave(copy, raw[c, at][:, :, a - at : a - at + n], rounded(c, a, n))

        def quantize(words, scale_bytes, source):
            nc.vector.quantize_mx(out=words.bitcast(FP8X4), scales=scale_bytes, in_=source)

        def quantize_x(c, a=0, n=CHUNK):
            quantize(codes[c][:, a : a + n], scales[c][:, a : a + n], rounded(c, a, n))

        sums = {}

        def product(c, k, number, a=0, n=CHUNK):
            mine = slice(k * P, (k + 1) * P)
            if number is None:
                target = sums[c, k, 0][:, a : a + n]
            else:
                sums[c, k, a] = bank(number, "sums%d_%d_%d" % (c, k, a))
                target = sums[c, k, a][:, 0:n]
            nc.tensor.matmul_mx(
                out=target,
                lhsT=w_codes[:, mine].bitcast(FP8X4),
                lhsT_scale=w_scales[:, mine],
                rhs=codes[c][:, a : a + n].bitcast(FP8X4),
                rhs_scale=scales[c][:, a : a + n],
                start=True,
                stop=True,
            )

        def activate(c, k, values, a=0, n=CHUNK, at=None):
            at = a if at is None else at
            source = sums[c, k, at][:, a - at : a - at + n]
            nc.scalar.activation(out=values[:, a : a + n], in_=source, func=GELU, bias=bias[:, k : k + 1])

        def place(c, k, values, weights):
            a, n = c * CHUNK, values.shape[1]
            where = offsets[:, a // STRIPE : (a + n) // STRIPE]
            nc.vector.tensor_tensor(windows[k][:].indirect(where), values, weights, ALU.mult)

        def store(k, c0, c1):
            nc.sync.dma_start(out_rows[k, :, c0:c1], windows[k][:, c0:c1])

        on_vector, on_scalar = (nc.vector.tensor_copy, RUN), (nc.scalar.copy, SCALAR_RUN)
        halves = (0, GROUP)

        nc.vector.memset(windows[A][:, 0:CHUNK], 0.0)
        clear(A, CHUNK, HALF)
        clear(B, SCALAR_CLEARS, SCALAR_CLEARS + CHUNK)
        clear(B, SCALAR_CLEARS + CHUNK, first_cleared)
        clear(A, HALF, S)
        clear(A, S, T - LATE_CLEARS_A)
        zeros = windows[A][:, 0:CHUNK].unsqueeze(1).to_broadcast([P, SCALAR_CLEARS // CHUNK, CHUNK])
        cleared = windows[B][:, 0:SCALAR_CLEARS].rearrange("p (n s) -> p n s", s=CHUNK)
        nc.scalar.activation(out=cleared, in_=zeros, func=GELU)
        nc.scalar.copy(
            out=w_grouped[:].rearrange("p (k c i t) -> p c t i k", k=BLOCKS, i=SCALAR_RUN, t=PACK),
            in_=w_raw[:].rearrange("p t (c i k) -> p c t i k", i=SCALAR_RUN, k=BLOCKS),
        )
        quantize(w_codes[:], w_scales[:], w_grouped[:])
        spread_gate(0, nc.scalar.copy)
        spread_gate(1, nc.vector.tensor_copy)

        def in_two(c, at, a, n):
            interleave_x(on_scalar, c, at, a, n // 2)
            interleave_x(on_scalar, c, at, a + n // 2, n // 2)

        interleave_x(on_vector, 0, 0, GROUP, GROUP)
        interleave_x(on_vector, 0, 0, SCALAR_OF_0, GROUP - SCALAR_OF_0)
        in_two(0, 0, 0, SCALAR_OF_0)
        spread_gate(2, nc.scalar.copy)
        spread_gate(3, nc.scalar.copy)
        values0_a = keep.tile([P, CHUNK], F32, name="values0_a")
        for a in reversed(halves):
            quantize_x(0, a, GROUP)
            product(0, A, 4 + a // GROUP, a, GROUP)
            activate(0, A, values0_a, a, GROUP)
        product(0, B, 6)
        interleave_x(on_vector, 1, 0, 0, GROUP)
        interleave_x(on_vector, 1, 0, GROUP, CUT_OF_1 - GROUP)
        quantize_x(1, 0, GROUP)
        quantize_x(1, GROUP, CUT_OF_1 - GROUP)
        product(1, A, 7, 0, GROUP)
        product(1, A, None, GROUP, CUT_OF_1 - GROUP)
        nc.gpsimd.memset(windows[B][:, first_cleared:last_cleared], 0.0)
        gate0, gate1 = gates[:, 0:CHUNK], gates[:, CHUNK:HALF]
        place(0, A, values0_a[:], gate0)
        nc.gpsimd.memset(windows[A][:, T - LATE_CLEARS_A : T], 0.0)
        in_two(1, CUT_OF_1, CUT_OF_1, CHUNK - CUT_OF_1)
        activate(0, B, values0_b)
        activate(1, A, values1_a, 0, CUT_OF_1)
        quantize_x(1, CUT_OF_1, CHUNK - CUT_OF_1)
        product(1, A, 0, CUT_OF_1, CHUNK - CUT_OF_1)
        product(1, B, 1)
        place(0, B, values0_b, gate0)
        nc.gpsimd.memset(windows[B][:, last_cleared:T], 0.0)
        in_two(2, 0, 0, GROUP)
        activate(1, A, values1_a, CUT_OF_1, CHUNK - CUT_OF_1)
        place(1, A, values1_a, gate1)
        store(A, 0, HALF)
        in_two(2, GROUP, GROUP, GROUP)
        quantize_x(2)
        product(2, A, 2)
        product(2, B, 3)
        activate(1, B, values1_b)
        place(1, B, values1_b, gate1)
        store(B, 0, HALF)

        interleave_x(on_scalar, 3, 0, 0, GROUP)
        in_two(3, GROUP, GROUP, GROUP)
        for a in halves:
            quantize_x(3, a, GROUP)
            product(3, A, 4 + a // GROUP, a, GROUP)
        product(3, B, 6)
        activate(2, A, values2_a)
        place(2, A, values2_a, gates[:, HALF : HALF + CHUNK])
        activate(2, B, values_b[:, 0:CHUNK])
        values3_a = keep.tile([P, CHUNK], F32, name="values3_a")
        for a in halves:
            activate(3, A, values3_a, a, GROUP)
        place(3, A, values3_a[:], gates[:, HALF + CHUNK : S])
        store(A, HALF, T)
        activate(3, B, values_b[:, CHUNK:HALF])
        place(2, B, values_b, gates[:, HALF:S])
        store(B, HALF, T)
